import numpy as np, ml_dtypes
CORES = [25,29,65,69,153,157,193,197]
N = 8
import mx_ref
BF = ml_dtypes.bfloat16
def entries(a):
    return np.ascontiguousarray(a.T).reshape(-1)
def table(e):
    return np.ascontiguousarray(np.reshape(e, (-1, 16)).T).astype(np.int32)
def pick(q, e):
    c = np.concatenate([q[0].reshape(128, -1, 4), np.zeros((128, 1, 4), np.uint8)], axis=1); s = np.concatenate([q[1], np.ones((16, 1), np.uint8)], axis=1)
    return (np.ascontiguousarray(c[:, e].reshape(128, -1)), np.ascontiguousarray(s[:, e]))
def join(*qs):
    return (np.concatenate([q[0] for q in qs], axis=1), np.concatenate([q[1] for q in qs], axis=1))
def put(q, e, v):
    c, s = q[0].reshape(128, -1, 4).copy(), q[1].copy(); c[:, e] = v[0].reshape(128, -1, 4); s[:, e] = v[1]
    return (c.reshape(128, -1), s)
def pk(c, s):
    return (np.ascontiguousarray(c), mx_ref.live(s))
def emit(q):
    return q[0], q[1]
def decode(q):
    o = []
    for b in range(4):
        e = np.zeros((128, 128, 4), np.float32); e[np.arange(128), np.arange(128), b] = 1
        o.append(mx_ref.matmul(mx_ref.quantize(e.reshape(128, 512).astype(BF)), q))
    return np.stack(o, axis=2).reshape(128, -1)
def cut(t, i, w=512):
    return t[:, w * i:w * i + w]
def f(rng, *shape):
    return mx_ref.flush((rng.standard_normal(shape, dtype=np.float32) * np.exp2(rng.integers(-2, 3, shape[:-1] + (1,)))).astype(BF))
def wide(rng, *shape, cols=0):
    v = rng.standard_normal(shape, dtype=np.float32) * np.exp2(rng.integers(-12, 13, shape)).astype(np.float32)
    if cols: v *= np.repeat(np.exp2(rng.integers(-cols, cols + 1, shape[:-2] + (1, shape[-1] // 4))) * (rng.random(shape[:-2] + (1, shape[-1] // 4)) > 0.0625), 4, axis=-1).astype(np.float32)
    return mx_ref.flush(v.astype(BF))
V, E, PAIR, CAP, R, O = 32, 128, 16, 8, 3, 2
def lift(v):
    v = np.array(v, np.float32)
    v[np.abs(v) < np.float32(2.0 ** -12)] = 0
    return v.astype(BF)
def lay(back):
    return np.stack([table(back[E * r:E * r + E]) for r in range(N)])
def links(rng):
    back = np.zeros(N * E, int)
    part = [rng.permutation(E).reshape(N, PAIR) + E * r for r in range(N)]
    for r in range(N):
        for h in range(r, N):
            a, c = part[r][h], part[h][r]
            if h == r: a, c = a[:PAIR // 2], a[PAIR // 2:]
            back[a] = c
            back[c] = a
    return lay(back)
def setup_inputs(rng):
    return {"b": lift(f(rng, N, 128, 4 * V)), "m": lift(f(rng, N, 128, 4 * E)), "u": f(rng, N, 128, 512), "w": f(rng, N, 128, 512 * O), "rev": links(rng)}
def setup_inputs_ties(rng):
    d = setup_inputs(rng)
    x = rng.integers(4, 8, (128, 1, 4)) * np.exp2(rng.integers(-2, 1, (128, 1, 4))) * rng.choice([-1.0, 1.0], (128, 1, 4))
    double = rng.permutation(N) < N // 2
    d["b"] = np.stack([np.repeat(x * (1 + double[r]), V, axis=1).reshape(128, 4 * V) for r in range(N)]).astype(np.float32).astype(BF)
    d["m"] = np.stack([np.repeat(x, E, axis=1).reshape(128, 4 * E) for r in range(N)]).astype(np.float32).astype(BF)
    return d
def setup_inputs_near(rng):
    d = setup_inputs(rng)
    p = 8 * rng.permutation(16)[:3] + rng.integers(0, 8, 3)
    t = rng.integers(0, 4, 3)
    i = np.arange(V)
    rows = [np.full(V, 32), 4 * (i % 8), 4 * (i // 8)]
    g = 1.0 - 2 * rng.integers(0, 2, N)
    b, m, u = np.array(d["b"]).reshape(N, 128, V, 4), np.array(d["m"]).reshape(N, 128, E, 4), np.array(d["u"])
    u[:, :, :4] = 0
    for k in range(3):
        b[:, p[k], :, t[k]] = np.broadcast_to(rows[k], (N, V)).astype(np.float32).astype(BF)
        m[:, p[k], :, t[k]] = 0
        u[:, p[k], t[k]] = (g * 2.0 ** (0, -19, -16)[k]).astype(np.float32).astype(BF)
    d["b"], d["m"], d["u"] = b.reshape(N, 128, 4 * V), m.reshape(N, 128, 4 * E), u
    return d
def setup_inputs_huge_order(rng):
    d = setup_inputs(rng)
    for k, n in (("b", V), ("m", E)):
        sign = np.repeat(1 - 2 * rng.integers(0, 2, (N, 1, n)), 4, axis=2)
        d[k] = ((1 + rng.random((N, 128, 4 * n))) * 2.0 ** 27 * sign).astype(np.float32).astype(BF)
    u = np.array(d["u"])
    u[:, :, :4] = ((1 + rng.random((N, 128, 4))) * 2.0 ** 29 * (1 - 2 * rng.integers(0, 2, (N, 1, 1)))).astype(np.float32).astype(BF)
    d["u"] = u
    for g in rng.permutation(16)[:2]:
        x = rng.integers(4, 8, (8, 1, 4)) * 2.0 ** 25 * rng.choice([-1.0, 1.0], (8, 1, 4))
        kind = rng.integers(-1, 2, (N, 1, E, 1))
        small = rng.integers(1, 8, (N, 8, E, 4)) * 0.25 * rng.choice([-1.0, 1.0], (N, 8, E, 4))
        nodes = x * (1 - 2 * rng.integers(0, 2, (N, 1, V, 1)))
        d["b"][:, 8 * g:8 * g + 8] = nodes.reshape(N, 8, 4 * V).astype(np.float32).astype(BF)
        d["m"][:, 8 * g:8 * g + 8] = np.where(kind == 0, small, x * kind).reshape(N, 8, 4 * E).astype(np.float32).astype(BF)
    return d
def setup_inputs_blocks(rng):
    d = setup_inputs(rng)
    spots = [np.arange(V).reshape(N, PAIR // 4)[rng.permutation(N)] + V * r for r in range(N)]
    back, keep, four = np.zeros(N * E, int), np.zeros(N * V, bool), np.arange(4)
    for r in range(N):
        for h in range(r, N):
            a, c = spots[r][h], rng.permutation(spots[h][r])
            if h == r: c = a
            for k in range(PAIR // 4):
                q = rng.permutation(4)
                if h == r:
                    back[4 * a[k] + q] = 4 * a[k] + q[[1, 0, 3, 2]]
                else:
                    back[4 * a[k] + four] = 4 * c[k] + q
                    back[4 * c[k] + q] = 4 * a[k] + four
            on = rng.integers(0, PAIR // 4)
            if (r + h) % 2 == 0:
                keep[a[on]] = True
                keep[c[on]] = True
            else:
                keep[a] = True
                keep[c] = True
    d["b"] = np.where(np.repeat(keep.reshape(N, 1, V), 4, axis=2), d["b"], np.zeros_like(d["b"]))
    d["m"] = np.where(np.repeat(keep.reshape(N, 1, V), 16, axis=2), d["m"], np.zeros_like(d["m"]))
    d["rev"] = lay(back)
    return d
def setup_inputs_spread(rng):
    d = {**setup_inputs(rng), "b": lift(wide(rng, N, 128, 4 * V, cols=6)), "m": lift(wide(rng, N, 128, 4 * E, cols=6))}
    u = np.array(d["u"])
    u[int(rng.integers(0, N)), :, :4] = 0
    return {**d, "u": u}
def check_inputs(d):
    bad = []
    for k, low, high in (("b", -12, 28), ("m", -12, 28), ("u", -30, 30), ("w", -30, 30)):
        v = np.abs(d[k].astype(np.float32))
        if not (np.isfinite(v).all() and ((v == 0) | (v >= 2.0 ** low) & (v <= 2.0 ** high)).all()): bad.append("a value of " + k)
    back = np.concatenate([entries(d["rev"][r]) for r in range(N)])
    if back.min() < 0 or back.max() >= N * E:
        bad.append("rev is out of range")
        return bad
    e = np.arange(N * E)
    if (back[back] != e).any() or (back == e).any(): bad.append("rev isn't made of pairs of different edges")
    if (np.bincount(e // E * N + back // E, minlength=N * N) != PAIR).any(): bad.append("edges of a pair of ranks")
    return bad
def reference(b, m, u, w, rev):
    y, up = np.zeros((N, 128, R * O * E), np.float32), np.zeros((N, 1, E), np.float32)
    oc, osc = np.zeros((N, 128, 4 * E), np.uint8), np.zeros((N, 16, E), np.uint8)
    back = np.concatenate([entries(rev[r]) for r in range(N)])
    e = np.arange(N * E)
    head = back // E
    others = np.array([[k for k in range(4) if k != j] for j in range(4)])
    come = back[4 * (e // 4)[:, None] + others[e % 4]]
    msg = mx_ref.quantize(np.concatenate([m[r] for r in range(N)], axis=1))
    dm = decode(msg).reshape(128, N * E, 4)
    db = decode(mx_ref.quantize(np.concatenate([b[r] for r in range(N)], axis=1))).reshape(128, N * V, 4)
    qu = [mx_ref.quantize(np.ascontiguousarray(u[r])) for r in range(N)]
    qw = [[mx_ref.quantize(np.ascontiguousarray(cut(w[r], o))) for o in range(O)] for r in range(N)]
    for t in range(R):
        z = db[:, e // 4]
        for j in range(3): z = z + dm[:, come[:, j]]
        z = z * np.float32(0.25)
        cand = mx_ref.quantize(np.ascontiguousarray(z.reshape(128, -1).astype(BF)))
        dc = decode(cand).reshape(128, N * E, 4)
        change = mx_ref.quantize(np.ascontiguousarray((dc - dm).reshape(128, -1).astype(BF)))
        taken = []
        for r in range(N):
            s = np.abs(mx_ref.matmul(qu[r], pick(change, np.arange(E * r, E * r + E)))[0]) + np.float32(0)
            for h in range(N):
                k = np.flatnonzero(head[E * r:E * r + E] == h)
                k = k[np.argsort(-s[k], kind="stable")[:CAP]]
                up[r, 0, k] += 1
                taken.append(E * r + k)
        taken = np.concatenate(taken)
        msg = put(msg, taken, pick(cand, taken))
        dm[:, taken] = dc[:, taken]
        for r in range(N):
            new = np.arange(E * r, E * r + E) if t == 0 else taken[N * CAP * r:N * CAP * r + N * CAP]
            now = pick(msg, new)
            for o in range(O):
                i = (t * O + o) * E
                if t > 0: y[r, :, i:i + E] = y[r, :, i - O * E:i - O * E + E]
                y[r][:, i + new - E * r] = mx_ref.matmul(qw[r][o], now)
    for r in range(N): oc[r], osc[r] = emit(pick(msg, np.arange(E * r, E * r + E)))
    return {"y": y, "oc": oc, "osc": osc, "up": up}

@@ -1,0 +1,463 @@
+from concourse.bass import DstId, RemoteDMATransfer
+from concourse.mybir import dt, AluOpType as A, AxisListType, ActivationFunctionType as F
+
+N, V, E, R, O, K = 8, 32, 128, 3, 2, 16
+X4, U8, U16, BF, F32, I32 = "float8_e4m3fn_x4", "uint8", "uint16", "bfloat16", "float32", "int32"
+SCRATCH = {}
+
+
+def _buf(name, cols, dtype, where="sbuf"):
+    SCRATCH[name] = (where, [128, cols], dtype)
+
+
+for _i in range(4):
+    _buf("zb%d" % _i, 512, F32, "psum")
+    _buf("db%d" % _i, 512, F32, "psum")
+for _n, _c, _d in (
+        ("wr", 10, I32), ("mb", 640, BF), ("uc", 4, BF), ("wt", 1024, BF),
+        ("one", 128, BF), ("idb", 128, BF), ("eb", 516, BF), ("nb", 516, BF), ("pb", 512, BF), ("gb", 512, BF), ("gb2", 512, BF), ("ub", 512, BF),
+        ("im16", 128, F32), ("ij", 128, BF),
+        ("ki", 8, I32),
+        ("kf", 8, F32),
+        ("cf", 96, F32),
+        ("li", 40, I32),
+        ("lff", 48, F32),
+        ("sm", 12, F32),
+        ("tt", 48, F32),
+        ("sgl", 2, U16), ("dupl", 16, U16), ("ls", 8, U16), ("lb", 8, U16), ("fd", 48, U16), ("lf", 24, U16), ("ln", 8, U16),
+        ("ah", 128, BF), ("hd", 128, BF), ("mk", 1024, BF), ("cu", 1024, BF), ("jk", 1024, BF),
+        ("ar", 128, F32), ("rb", 128, F32), ("js", 512, BF), ("asl", 128, BF), ("slb", 128, BF),
+        ("ft", 24, F32), ("fk", 24, F32), ("dk", 768, BF), ("dkt", 768, BF),
+        ("pob", 128, BF), ("pd", 256, BF), ("pdt", 256, BF), ("ups", 128, F32), ("upn", 128, F32),
+        ("z", 512, BF), ("dd", 512, BF), ("sx", 128, F32)):
+    _buf(_n, _c, _d)
+for _n, _c in (("qmb", 160), ("bb", 128), ("ep", 512), ("en", 512), ("pc", 128), ("qg", 128), ("qg2", 128), ("qu", 128), ("qw", 256), ("qd", 128),
+               ("mw0", 256), ("mw1", 256), ("mw2", 256), ("mw3", 128), ("iw0", 256), ("iw1", 256), ("iw2", 128),
+               ("rm0", 32), ("rc0", 32), ("rc1", 32), ("f0", 384), ("f1", 384), ("f2", 384), ("nt0", 128), ("nt1", 128), ("nt2", 128)):
+    _buf(_n, _c, X4)
+    _buf(_n + "_s", _c, U8)
+for _t in range(R):
+    _buf("lst%d" % _t, 16, U16)
+    _buf("ys%d" % _t, 256, F32)
+for _t in range(R - 1):
+    _buf("rl%d" % _t, 8, U16)
+    _buf("rq%d" % _t, 2, U16)
+
+STAGES = ["m0", "m0s", "c0", "c0s", "l0", "c1", "c1s", "l1"]
+SEMAPHORES = ["qv", "qs", "qt", "qg", "ls", "ldr", "ldm", "ldu", "ldw", "hm0", "hc0", "hc1", "hl0", "hl1", "st"]
+SEMAPHORES += ["a_" + s for s in STAGES] + ["r_" + s for s in STAGES]
+SPLIT = ("m0", "m0s", "l0", "l1")
+
+
+def direct(T, topo, c):
+    return [d for d in T.cores if d != c and topo.may_write(c, d)]
+
+
+def cross(T, topo, c):
+    return [d for d in T.cores if d != c and not topo.may_write(c, d)]
+
+
+def relay(T, topo, c, d):
+    own = [x for x in topo.cores_of(c) if T.rank_of(x) is None and topo.may_write(x, d)]
+    near = [x for x in own if topo.die(x) == topo.die(d)] or own
+    same = [x for x in cross(T, topo, c) if topo.die(x) == topo.die(d)]
+    return near[same.index(d) % len(near)]
+
+
+def pow2(n):
+    k = 1
+    while 2 * k <= n:
+        k *= 2
+    return k
+
+
+def share(topo, c, dsts):
+    off = [d for d in dsts if d not in topo.cores_of(c)]
+    on = [d for d in dsts if d in topo.cores_of(c)]
+    out = {}
+    every = topo.engines(c, on[0]) if on else topo.engines(c, off[0])
+    per = pow2(len(every) // len(dsts))
+    used = []
+    for i, d in enumerate(off):
+        out[d] = topo.engines(c, d)[per * i:per * i + per]
+        used += out[d]
+    left = [e for e in every if e not in used]
+    per = pow2(len(left) // len(on)) if on else 0
+    for i, d in enumerate(on):
+        out[d] = left[per * i:per * i + per]
+    return out
+
+
+def calls(T, topo, c, stage):
+    near = [(d, d) for d in direct(T, topo, c)]
+    far = [(d, relay(T, topo, c, d)) for d in cross(T, topo, c)]
+    out = []
+    for part in ([far, near] if stage in SPLIT else [far + near]):
+        if part:
+            e = share(topo, c, [x for _, x in part])
+            out.append([(d, x, e[x]) for d, x in part])
+    return out
+
+
+def bits(engines):
+    return sum(1 << e for e in engines)
+
+
+def peers(T, topo, c):
+    return [x for x in topo.cores_of(c) if T.rank_of(x) is not None]
+
+
+def landed(T, topo, c, stage):
+    n = 0
+    for s in T.cores:
+        if s != c:
+            n += sum(len(e) for part in calls(T, topo, s, stage) for _, x, e in part if x == c)
+            if T.rank_of(c) is not None and not topo.may_write(s, c) and s == peers(T, topo, s)[0]:
+                n += len(topo.engines(relay(T, topo, s, c), c))
+    return n
+
+
+def relay_program(g, core, T, topo):
+    mine = peers(T, topo, core)
+    todo = [d for d in cross(T, topo, mine[0]) if relay(T, topo, mine[0], d) == core]
+    if not todo:
+        return
+    d = todo[0]
+    rid, pid = topo.addr(d, core)
+    r0, n = T.rank_of(mine[0]), len(mine)
+    sent = 0
+    for st in STAGES:
+        t = int(st[1])
+        tail = "_s" if st.endswith("s") else ""
+        if st[0] == "l":
+            src, dst = T["rq%d" % t][:], T["rl%d" % t][:, r0:r0 + n]
+        else:
+            col = K * r0 + (E if st[0] == "c" else 0)
+            src, dst = T["r" + st[:2] + tail][:], T["iw%d" % t + tail][:, col:col + K * n]
+            if not tail:
+                src, dst = src.bitcast(dt.uint8), dst.bitcast(dt.uint8)
+        e = topo.engines(core, d)
+        g.wait_ge(T.sem["r_" + st], landed(T, topo, core, st))
+        g.remote_dma(dst, src, T.sem["a_" + st], T.sem["ls"], pid, rid, bits(e))
+        sent += len(e)
+    g.wait_ge(T.sem["ls"], sent)
+
+
+def rank_program(g, core, T, topo):
+    rank = T.rank_of(core)
+    if rank is None:
+        if peers(T, topo, core):
+            relay_program(g, core, T, topo)
+        return
+    q = {"v": g.vector, "s": g.scalar, "t": g.tensor, "g": g, "y": g.sync}
+    count, seen, wrote, read, want = {}, {}, {}, {}, {}
+
+    def need(k, toks):
+        for s, n in toks:
+            if not (k == "t" and s == "qt") and seen.get((k, s), 0) < n:
+                want[s] = max(want.get(s, 0), n)
+
+    def waits(k, rd, wr):
+        want.clear()
+        for r in rd:
+            need(k, wrote.get(r, []))
+        for w in wr:
+            need(k, wrote.get(w, []))
+            need(k, read.get(w, []))
+        for s, n in want.items():
+            q[k].wait_ge(T.sem[s], n)
+            seen[(k, s)] = n
+
+    def note(tok, rd, wr):
+        for r in rd:
+            read.setdefault(r, []).append(tok)
+        for w in wr:
+            wrote[w] = [tok]
+            read[w] = []
+
+    def op(k, fn, rd=(), wr=()):
+        waits(k, rd, wr)
+        s = "q" + k
+        fn().then_inc(T.sem[s], 1)
+        count[s] = count.get(s, 0) + 1
+        note((s, count[s]), rd, wr)
+
+    def dmas(parts, s, rd=(), wr=()):
+        for k in sorted({p[0] for p in parts}):
+            waits(k, rd, wr)
+        for k, o, i in parts:
+            q[k].dma_start(o, i).then_inc(T.sem[s], 16)
+            count[s] = count.get(s, 0) + 16
+        note((s, count[s]), rd, wr)
+
+    v, sc, te = g.vector, g.scalar, g.tensor
+    u8, u32 = dt.uint8, dt.uint32
+
+    def tsc(o, i, s1, s2, o1, o2, rd, wr):
+        if o2 is None:
+            op("v", lambda: v.tensor_scalar(o, i, s1, None, o1), rd, wr)
+        else:
+            op("v", lambda: v.tensor_scalar(o, i, s1, s2, o1, o2), rd, wr)
+
+    def cp(o, i, rd, wr):
+        op("v", lambda: v.tensor_copy(o, i), rd, wr)
+
+    def ttn(o, a, b, f, rd, wr):
+        op("v", lambda: v.tensor_tensor(o, a, b, f), rd, wr)
+
+    def fill(o, x, rd, wr):
+        op("v", lambda: v.memset(o, x), rd, wr)
+
+    def turn(o, i, rd, wr):
+        op("v", lambda: v.transpose(o, i), rd, wr)
+
+    def act(o, i, fn, rd, wr, **kw):
+        op("s", lambda: sc.activation(o, i, fn, **kw), rd, wr)
+
+    def iota(o, pattern, ch, wr):
+        op("g", lambda: g.iota(o, pattern, 0, ch, allow_small_or_imprecise_dtypes=True), (), [wr])
+
+    def quant(name, a, b, tile, x, rd, wr):
+        op("v", lambda: v.quantize_mx(T[name][:, a:b], T[name + "_s"][:, a:b], T[tile][:, x:x + 4 * (b - a)]), rd, wr)
+
+    def pick(out, a, src, c, d, off, e, codes, scales, lists, wc, ws):
+        op("v", lambda: v.tensor_copy(T[out][:, a:a + 128].bitcast(u32), T[src][:, c:d].bitcast(u32).indirect(T[off][:, e:e + 8])), codes + lists, [wc])
+        op("s", lambda: sc.activation(T[out + "_s"][:, a:a + 128], T[src + "_s"][:, c:d].indirect(T[off][:, e:e + 8]), F.Copy), scales + lists, [ws])
+
+    def mm(bank, ln, la, rn, ra, start, stop, rd):
+        op("t", lambda: te.matmul_mx(T[bank][:, 0:128], T[ln][:, la:la + 128], T[ln + "_s"][:, la:la + 128],
+                                     T[rn][:, ra:ra + 128], T[rn + "_s"][:, ra:ra + 128], start, stop), rd, [bank])
+
+    parts = []
+    for a in range(4):
+        for d in range(2):
+            parts.append(("ys"[d], T.wr[32 * a + 16 * d:32 * a + 16 * d + 16, 1 - d:9 - d], T.rev[:, :]))
+    dmas(parts, "ldr", (), ["wr"])
+    dmas([("y", T.mb[:, 0:512], T.m[:, :]), ("s", T.mb[:, 512:640], T.b[:, :])], "ldm", (), ["mb"])
+    dmas([("y", T.uc[:, :], T.u[:, 0:4])], "ldu", (), ["uc"])
+    dmas([("y", T.wt[:, :], T.w[:, :])], "ldw", (), ["wt"])
+
+    fill(T.one[:, :], 1.0, (), ["one"])
+    fill(T.eb[:, :], 0.0, (), ["eb"])
+    fill(T.nb[:, :], 0.0, (), ["nb"])
+    fill(T.pb[:, :], 0.0, (), ["pb"])
+    op("g", lambda: g.iota(T.ki[:, 0:2], [[0, 2]], 0, 1), (), ["ip"])
+    op("g", lambda: g.affine_select(T.idb[:, :], T.one[:, :], [[-1, 128]], A.is_equal, 0.0, 0, 1), ["one"], ["idb"])
+    iota(T.im16[:, :], [[0, 8], [1, 16]], 0, "im16")
+    iota(T.cf[:, 0:16], [[0, 2], [1, 8]], 0, "c8")
+    iota(T.cf[:, 16:32], [[16, 8], [0, 2]], 0, "h16")
+    iota(T.ij[:, :], [[1, 128]], 0, "ij")
+    tsc(T.ki[:, 2:4], T.ki[:, 0:2], 15, None, A.bitwise_and, None, ["ip"], ["kci"])
+    tsc(T.ki[:, 4:6], T.ki[:, 0:2], 4, None, A.logical_shift_right, None, ["ip"], ["gci"])
+    cp(T.sgl[:, :], T.ki[:, 0:2], ["ip"], ["sgl"])
+    cp(T.kf[:, 0:2], T.ki[:, 2:4], ["kci"], ["kcf"])
+    cp(T.kf[:, 2:4], T.ki[:, 4:6], ["gci"], ["gcf"])
+    tsc(T.kf[:, 4:6], T.ki[:, 2:4], 0.5, None, A.add, None, ["kci"], ["khf"])
+    k16, g16, k05 = T.kf[:, 0:1], T.kf[:, 2:3], T.kf[:, 4:5]
+    cp(T.eb[:, 3:515:4], T.idb[:, :], ["idb"], ["eb"])
+    act(T.nb[:, 3:515:4], T.idb[:, :], F.Copy, ["idb"], ["nb"], scale=-1.0)
+    for b in range(4):
+        quant("ep", 128 * b, 128 * b + 128, "eb", 3 - b, ["eb"], ["ep"])
+
+    tsc(T.li[:, 0:4], T.wr[:, 1:9:2], 7, None, A.logical_shift_right, None, ["wr"], ["h4i"])
+    cp(T.lff[:, 0:4], T.li[:, 0:4], ["h4i"], ["h4f"])
+
+    def spread(dst, col, name, rd):
+        for b in range(4):
+            x = T.lff[:, col + b:col + b + 1]
+            if b % 2:
+                act(T[dst][:, 32 * b:32 * b + 32], T.one[:, 0:32], F.Copy, ["one", rd], [dst + ".%d" % b], scale=x)
+            else:
+                tsc(T[dst][:, 32 * b:32 * b + 32], T.one[:, 0:32], x, None, A.mult, None, ["one", rd], [dst + ".%d" % b])
+        turn(T[name][:, :], T[dst][:, :], [dst + ".%d" % b for b in range(4)], [name])
+
+    spread("ah", 0, "hd", "h4f")
+
+    def mask(h):
+        tsc(T.mk[:, E * h:E * h + E], T.hd[:, :], float(h), None, A.is_equal, None, ["hd"], ["mk%d" % h])
+
+    mask(0)
+    mask(1)
+    for h in range(N):
+        s0, s1 = E * h, E * h + E
+        op("v", lambda: v.tensor_tensor_scan(T.cu[:, s0:s1], T.mk[:, s0:s1], T.mk[:, s0:s1], 0.0, A.add, A.max), ["mk%d" % h], ["cu%d" % h])
+        if h + 2 < N:
+            mask(h + 2)
+        act(T.jk[:, s0:s1], T.cu[:, s0:s1], F.Sign, ["cu%d" % h, "khf"], ["jk%d" % h, "acc%d" % h], scale=-1.0, bias=k05, accum_out=T.lff[:, 16 + h:17 + h])
+    quant("qmb", 0, 160, "mb", 0, ["mb"], ["qmb"])
+    tsc(T.ls[:, :], T.lff[:, 16:24], 0.5, 64.0, A.mult, A.add, ["acc%d" % h for h in range(N)], ["ls"])
+    pick("mw0", 0, "qmb", 0, 128, "ls", 0, ["qmb"], ["qmb"], ["ls"], "mw0.m", "mw0.m_s")
+
+    def view(name, a, n, codes):
+        x = T[name][:, a:a + n]
+        return x.bitcast(u8) if codes else x
+
+    def send(stage, src, rd):
+        t, codes = int(stage[1]), stage[0] != "l" and not stage.endswith("s")
+        tail = "_s" if stage.endswith("s") else ""
+        i = peers(T, topo, core).index(core)
+        waits("g", rd, ())
+        for part in calls(T, topo, core, stage):
+            tr = []
+            for d, x, e in part:
+                if stage[0] == "l":
+                    dst = T["rl%d" % t][:, rank:rank + 1] if x == d else T["rq%d" % t][:, i:i + 1]
+                elif x == d:
+                    dst = view("iw%d" % t + tail, K * rank + (E if stage[0] == "c" else 0), K, codes)
+                else:
+                    dst = view("r" + stage[:2] + tail, K * i, K, codes)
+                rid, pid = topo.addr(x, core)
+                tr.append(RemoteDMATransfer(dst_ids=[DstId(rid=rid, pnc=pid)], dma_engine_mask=bits(e),
+                                            remote_sem=T.sem[("a_" if x == d else "r_") + stage], src=src(T.rank_of(d)), dst=dst))
+                count["ls"] = count.get("ls", 0) + len(e)
+            g.remote_dma_fused(tr, local_sem=T.sem["ls"])
+        count["a_" + stage] = landed(T, topo, core, stage)
+        return ("a_" + stage, count["a_" + stage])
+
+    def columns(t, base, stage, rd):
+        m = "mw%d" % t
+        tc = send(stage, lambda h: view(m, base + K * h, K, True), [rd])
+        ts = send(stage + "s", lambda h: view(m + "_s", base + K * h, K, False), [rd + "_s"])
+        at = base + K * rank
+        dmas([("y", view("iw%d" % t, at, K, True), view(m, at, K, True)),
+              ("y", view("iw%d_s" % t, at, K, False), view(m + "_s", at, K, False))], "h" + stage, [rd, rd + "_s"], ["home"])
+        part = "iw%d" % t + (".c" if base else ".m")
+        wrote[part], wrote[part + "_s"] = [tc] + wrote["home"], [ts] + wrote["home"]
+        del wrote["home"]
+
+    columns(0, 0, "m0", "mw0.m")
+
+    cp(T.lff[:, 4:8], T.wr[:, 1:9:2], ["wr"], ["r4f"])
+    spread("ar", 4, "rb", "r4f")
+    for b in range(4):
+        act(T.js[:, 128 * b:128 * b + 128], T.rb[:, :], F.Sign, ["rb", "r4f"], ["js%d" % b, "sa%d" % b], scale=-1.0, bias=T.lff[:, 4 + b:5 + b], accum_out=T.lff[:, 8 + b:9 + b])
+    cp(T.li[:, 8:16], T.ls[:, :], ["ls"], ["lsi"])
+    tsc(T.li[:, 16:24], T.li[:, 8:16], 3, None, A.bitwise_and, None, ["lsi"], ["lqi"])
+    tsc(T.li[:, 24:32], T.li[:, 8:16], 124, None, A.bitwise_and, None, ["lsi"], ["l4i"])
+    tsc(T.li[:, 32:40], T.li[:, 8:16], 2, None, A.logical_shift_right, None, ["lsi"], ["lbi"])
+    cp(T.lff[:, 32:40], T.li[:, 16:24], ["lqi"], ["lqf"])
+    cp(T.lff[:, 40:48], T.li[:, 24:32], ["l4i"], ["lbf"])
+    cp(T.lb[:, :], T.li[:, 32:40], ["lbi"], ["lb"])
+    for k in range(3):
+        tsc(T.ft[:, 8 * k:8 * k + 8], T.lff[:, 32:40], float(k), float(k), A.is_le, A.add, ["lqf"], ["ft%d" % k])
+    for k in range(3):
+        ttn(T.fk[:, 8 * k:8 * k + 8], T.ft[:, 8 * k:8 * k + 8], T.lff[:, 40:48], A.add, ["ft%d" % k, "lbf"], ["fk"])
+    cp(T.fd[:, 0:48:2], T.fk[:, :], ["fk"], ["fd0"])
+    cp(T.fd[:, 1:48:2], T.fk[:, :], ["fk"], ["fd1"])
+    tsc(T.lff[:, 12:16], T.lff[:, 8:12], 0.5, 63.5, A.mult, A.add, ["sa%d" % b for b in range(4)], ["s4"])
+    spread("asl", 12, "slb", "s4")
+    for k in range(3):
+        d0, d1 = 256 * k, 256 * k + 256
+        cp(T.dk[:, d0:d1], T.slb[:, :].indirect(T.fd[:, 16 * k:16 * k + 16]), ["slb", "fd0", "fd1"], ["dk%d" % k])
+        turn(T.dkt[:, d0:d1], T.dk[:, d0:d1], ["dk%d" % k], ["dkt%d" % k])
+        cp(T.lf[:, 8 * k:8 * k + 8], T.dkt[:, d0:d1:32], ["dkt%d" % k], ["lf%d" % k])
+    pick("bb", 0, "qmb", 128, 160, "lb", 0, ["qmb"], ["qmb"], ["lb"], "bb", "bb_s")
+    for b in range(4):
+        quant("en", 128 * b, 128 * b + 128, "nb", 3 - b, ["nb"], ["en"])
+    for t in range(4):
+        tsc(T.ub[:, t:512:4], T.one[:, :], T.uc[:, t:t + 1], None, A.mult, None, ["one", "uc"], ["ub%d" % t])
+    quant("qu", 0, 128, "ub", 0, ["ub%d" % t for t in range(4)], ["qu"])
+
+    tsc(T.pb[:, 0:512:4], T.im16[:, :], k16, 128.0, A.is_equal, A.mult, ["im16", "kcf", "pb"], ["pb0"])
+    fill(T.pb[0:1, 1:512:4], 1.0, ["pb"], ["pb1"])
+    cp(T.pb[0:1, 2:512:4], T.im16[0:1, :], ["im16", "pb"], ["pb2"])
+    fill(T.pb[:, 3:512:4], 1.0, ["pb"], ["pb3"])
+    quant("pc", 0, 128, "pb", 0, ["pb0", "pb1", "pb2", "pb3"], ["pc"])
+    fill(T.gb[:, :], 0.0, (), ["gb"])
+    fill(T.gb2[:, :], 0.0, (), ["gb2"])
+    fill(T.gb[0:1, 1:32:4], float(K * rank), ["gb"], ["gb1"])
+    cp(T.gb[0:1, 33:64:4], T.cf[0:1, 16:32:2], ["h16", "gb"], ["gb3"])
+    fill(T.gb[0:1, 2:64:4], 1.0, ["gb"], ["gb4"])
+    tsc(T.cf[:, 32:48], T.cf[:, 0:16], g16, 8.0, A.is_equal, A.mult, ["c8", "gcf"], ["hm"])
+    tsc(T.cf[:, 48:64], T.im16[:, 0:16], k16, None, A.is_lt, None, ["im16", "kcf"], ["lt"])
+    tsc(T.cf[:, 64:80], T.cf[:, 48:64], -2.0 ** -24, 1.0, A.mult, A.add, ["lt"], ["mth"])
+    tsc(T.cf[:, 80:96], T.cf[:, 48:64], -2.0 ** -120, None, A.mult, None, ["lt"], ["bth"])
+    fill(T.sm[:, 4:5], 0.0, (), ["cnt0"])
+
+    def prefill_m(t):
+        for b in range(4):
+            mm("db%d" % b, "en", 128 * b, "mw%d" % t, 0, True, False, ["en", "mw%d.m" % t, "mw%d.m_s" % t])
+
+    def prefill_b():
+        for b in range(4):
+            mm("zb%d" % b, "ep", 128 * b, "bb", 0, True, False, ["ep", "bb", "bb_s"])
+
+    prefill_b()
+    prefill_m(0)
+    cp(T.pob[:, :].indirect(T.ls[:, :]), T.ij[:, :], ["ls", "ij"], ["pob"])
+    tsc(T.dupl[:, :], T.cf[:, 16:32], k16, None, A.add, None, ["h16", "kcf"], ["dupl"])
+    cp(T.pd[:, :], T.pob[:, :].indirect(T.dupl[:, :]), ["pob", "dupl"], ["pd"])
+    turn(T.pdt[:, :], T.pd[:, :], ["pd"], ["pdt"])
+    cp(T.ln[:, :], T.pdt[:, 0:256:32], ["pdt"], ["ln"])
+    quant("qw", 0, 256, "wt", 0, ["wt"], ["qw"])
+
+    for t in range(R):
+        iw, mw, f, lst = "iw%d" % t, "mw%d" % t, "f%d" % t, "lst%d" % t
+        nw, nt, ys, last = "mw%d" % (t + 1), "nt%d" % t, "ys%d" % t, t == R - 1
+        for k in range(3):
+            pick(f, 128 * k, iw, 0, 128, "lf", 8 * k, [iw + ".m"], [iw + ".m_s"], ["lf%d" % k], f + ".%d" % k, f + "s.%d" % k)
+        for k in range(3):
+            for b in range(4):
+                mm("zb%d" % b, "ep", 128 * b, f, 128 * k, False, k == 2, ["ep", f + ".%d" % k, f + "s.%d" % k])
+        for b in range(4):
+            if b % 2 == 0:
+                tsc(T.z[:, b:512:4], T["zb%d" % b][:, 0:128], 0.25, None, A.mult, None, ["zb%d" % b], ["z%d" % b])
+            else:
+                act(T.z[:, b:512:4], T["zb%d" % b][:, 0:128], F.Copy, ["zb%d" % b], ["z%d" % b], scale=0.25)
+        quant(mw, 128, 256, "z", 0, ["z%d" % b for b in range(4)], [mw + ".c", mw + ".c_s"])
+        for b in range(4):
+            mm("db%d" % b, "ep", 128 * b, mw, 128, False, True, ["ep", mw + ".c"])
+        if not last:
+            columns(t, E, "c%d" % t, mw + ".c")
+        for b in range(4):
+            if b % 2 == 0:
+                cp(T.dd[:, b:512:4], T["db%d" % b][:, 0:128], ["db%d" % b], ["dd%d" % b])
+            else:
+                act(T.dd[:, b:512:4], T["db%d" % b][:, 0:128], F.Copy, ["db%d" % b], ["dd%d" % b])
+        quant("qd", 0, 128, "dd", 0, ["dd%d" % b for b in range(4)], ["qd"])
+        mm("zb1", "qu", 0, "qd", 0, True, True, ["qu", "qd"])
+        mm("zb0", "qd", 0, "qu", 0, True, True, ["qu", "qd"])
+        act(T.sx[:, :], T.zb1[:, 0:128], F.Abs, ["zb1"], ["sx"])
+        op("v", lambda: v.tensor_reduce(T.sm[:, 0:1], T.zb0[:, 0:2], AxisListType.X, A.max, apply_absolute_value=True), ["zb0"], ["sc"])
+        tsc(T.tt[:, 0:16], T.cf[:, 64:80], T.sm[:, 0:1], None, A.mult, None, ["mth", "sc"], ["th0"])
+        ttn(T.tt[:, 16:32], T.tt[:, 0:16], T.cf[:, 80:96], A.add, ["th0", "bth"], ["th"])
+        ttn(T.tt[:, 32:48], T.sx[:, :].indirect(T.sgl[:, 0:1]), T.tt[:, 16:32], A.is_gt, ["sx", "sgl", "th"], ["kk"])
+        op("v", lambda: v.tensor_reduce(T.sm[:, 2:3], T.tt[:, 32:48], AxisListType.X, A.add), ["kk"], ["rk"])
+        tsc(T.gb[:, 0:64:4], T.cf[:, 32:48], T.sm[:, 2:3], None, A.is_gt, None, ["hm", "rk", "gb"], ["gb0"])
+        quant("qg", 0, 128, "gb", 0, ["gb0", "gb1", "gb3", "gb4"], ["qg"])
+        mm("zb2", "pc", 0, "qg", 0, True, True, ["pc", "qg"])
+        tsc(T.sm[:, 5 + t:6 + t], T.sm[:, 2:3], 8.0, T.sm[:, 4 + t:5 + t], A.is_lt, A.add, ["rk", "cnt%d" % t], ["cnt%d" % (t + 1)])
+        cp(T[lst][:, :], T.zb2[:, 0:16], ["zb2"], [lst])
+        if not last:
+            tl = send("l%d" % t, lambda h: T[lst][:, h:h + 1], [lst])
+            dmas([("y", T["rl%d" % t][:, rank:rank + 1], T[lst][:, rank:rank + 1])], "hl%d" % t, [lst], ["home"])
+            wrote["rl%d" % t] = [tl] + wrote.pop("home")
+        else:
+            act(T.gb2[:, 3:512:4], T.idb[:, :], F.Copy, ["idb", "gb2", "cnt%d" % R], ["gb2d"], scale=T.sm[:, 4 + R:5 + R])
+        pick(nw, 0, mw, 0, 256, lst, 8, [mw + ".m", mw + ".c"], [mw + ".m_s", mw + ".c_s"], [lst], nw + ".m", nw + ".m_s")
+        if last:
+            quant("qg2", 0, 128, "gb2", 0, ["gb2d"], ["qg2"])
+            mm("zb3", "pc", 0, "qg2", 0, True, True, ["pc", "qg2"])
+        else:
+            prefill_m(t + 1)
+        pick(nt, 0, nw, 0, 128, "ln", 0, [nw + ".m"], [nw + ".m_s"], ["ln"], nt, nt + "_s")
+        if last:
+            dmas([("y", T.oc[:, :], view(nt, 0, 128, True))], "st", [nt], ())
+            act(T.ups[:, :], T.zb3[:, 0:128], F.Copy, ["zb3"], ["ups"])
+            dmas([("y", T.osc[4 * k:4 * k + 4, :], T[nt + "_s"][32 * k:32 * k + 4, :]) for k in range(4)], "st", [nt + "_s"], ())
+            cp(T.upn[:, :], T.ups[:, :].indirect(T.ln[:, :]), ["ups", "ln"], ["upn"])
+            dmas([("y", T.up[:, :], T.upn[0:1, :])], "st", ["upn"], ())
+        for o in range(O):
+            mm("zb%d" % o, "qw", 128 * o, nt, 0, True, True, ["qw", nt, nt + "_s"])
+        act(T[ys][:, 0:128], T.zb0[:, 0:128], F.Copy, ["zb0"], [ys + ".0"])
+        cp(T[ys][:, 128:256], T.zb1[:, 0:128], ["zb1"], [ys + ".1"])
+        if not last:
+            prefill_b()
+            dmas([("y", T.y[:, 256 * t:256 * t + 256], T[ys][:, :])], "st", [ys + ".0", ys + ".1"], ())
+            ni = "iw%d" % (t + 1)
+            pick(ni, 0, iw, 0, 256, "rl%d" % t, 0, [iw + ".m", iw + ".c"], [iw + ".m_s", iw + ".c_s"], ["rl%d" % t], ni + ".m", ni + ".m_s")
+        else:
+            dmas([("s", T.y[:, 256 * t:256 * t + 128], T[ys][:, 0:128])], "st", [ys + ".0"], ())
+            dmas([("y", T.y[:, 256 * t + 128:256 * t + 256], T[ys][:, 128:256])], "st", [ys + ".1"], ())
+    for s, n in sorted(count.items()):
+        g.wait_ge(T.sem[s], n)

@@ -16,12 +16,12 @@ for _i in range(4):
 for _n, _c, _d in (
         ("wr", 10, I32), ("mb", 640, BF), ("uc", 4, BF), ("wt", 1024, BF),
         ("one", 128, BF), ("idb", 128, BF), ("eb", 516, BF), ("nb", 516, BF), ("pb", 512, BF), ("gb", 512, BF), ("gb2", 512, BF), ("ub", 512, BF),
-        ("im16", 128, F32), ("ij", 128, BF),
+        ("im16", 128, F32), ("pa", 128, F32), ("ij", 128, BF),
         ("ki", 8, I32),
         ("kf", 8, F32),
-        ("cf", 96, F32),
+        ("cf", 112, F32),
         ("li", 40, I32),
-        ("lff", 48, F32),
+        ("lff", 52, F32),
         ("sm", 12, F32),
         ("tt", 48, F32),
         ("sgl", 2, U16), ("dupl", 16, U16), ("ls", 8, U16), ("lb", 8, U16), ("fd", 48, U16), ("lf", 24, U16), ("ln", 8, U16),
@@ -117,6 +117,15 @@ def landed(T, topo, c, stage):
     return n
 
 
+def view(T, name, a, n, codes):
+    x = T[name][:, a:a + n]
+    return x.bitcast(dt.uint8) if codes else x
+
+
+def kind(stage):
+    return int(stage[1]), "_s" if stage.endswith("s") else "", stage[0] != "l" and not stage.endswith("s"), E if stage[0] == "c" else 0
+
+
 def relay_program(g, core, T, topo):
     mine = peers(T, topo, core)
     todo = [d for d in cross(T, topo, mine[0]) if relay(T, topo, mine[0], d) == core]
@@ -124,23 +133,16 @@ def relay_program(g, core, T, topo):
         return
     d = todo[0]
     rid, pid = topo.addr(d, core)
-    r0, n = T.rank_of(mine[0]), len(mine)
-    sent = 0
+    r0, n, e = T.rank_of(mine[0]), len(mine), topo.engines(core, d)
     for st in STAGES:
-        t = int(st[1])
-        tail = "_s" if st.endswith("s") else ""
+        t, tail, codes, base = kind(st)
         if st[0] == "l":
-            src, dst = T["rq%d" % t][:], T["rl%d" % t][:, r0:r0 + n]
+            src, dst = T["rq%d" % t][:, 0:n], T["rl%d" % t][:, r0:r0 + n]
         else:
-            col = K * r0 + (E if st[0] == "c" else 0)
-            src, dst = T["r" + st[:2] + tail][:], T["iw%d" % t + tail][:, col:col + K * n]
-            if not tail:
-                src, dst = src.bitcast(dt.uint8), dst.bitcast(dt.uint8)
-        e = topo.engines(core, d)
+            src, dst = view(T, "r" + st[:2] + tail, 0, K * n, codes), view(T, "iw%d" % t + tail, base + K * r0, K * n, codes)
         g.wait_ge(T.sem["r_" + st], landed(T, topo, core, st))
         g.remote_dma(dst, src, T.sem["a_" + st], T.sem["ls"], pid, rid, bits(e))
-        sent += len(e)
-    g.wait_ge(T.sem["ls"], sent)
+    g.wait_ge(T.sem["ls"], len(STAGES) * len(e))
 
 
 def rank_program(g, core, T, topo):
@@ -191,7 +193,7 @@ def rank_program(g, core, T, topo):
         note((s, count[s]), rd, wr)
 
     v, sc, te = g.vector, g.scalar, g.tensor
-    u8, u32 = dt.uint8, dt.uint32
+    u32 = dt.uint32
 
     def tsc(o, i, s1, s2, o1, o2, rd, wr):
         if o2 is None:
@@ -238,40 +240,45 @@ def rank_program(g, core, T, topo):
     dmas([("y", T.wt[:, :], T.w[:, :])], "ldw", (), ["wt"])
 
     fill(T.one[:, :], 1.0, (), ["one"])
-    fill(T.eb[:, :], 0.0, (), ["eb"])
-    fill(T.nb[:, :], 0.0, (), ["nb"])
-    fill(T.pb[:, :], 0.0, (), ["pb"])
     op("g", lambda: g.iota(T.ki[:, 0:2], [[0, 2]], 0, 1), (), ["ip"])
     op("g", lambda: g.affine_select(T.idb[:, :], T.one[:, :], [[-1, 128]], A.is_equal, 0.0, 0, 1), ["one"], ["idb"])
     iota(T.im16[:, :], [[0, 8], [1, 16]], 0, "im16")
     iota(T.cf[:, 0:16], [[0, 2], [1, 8]], 0, "c8")
     iota(T.cf[:, 16:32], [[16, 8], [0, 2]], 0, "h16")
     iota(T.ij[:, :], [[1, 128]], 0, "ij")
+    fill(T.eb[:, :], 0.0, (), ["eb"])
     tsc(T.ki[:, 2:4], T.ki[:, 0:2], 15, None, A.bitwise_and, None, ["ip"], ["kci"])
     tsc(T.ki[:, 4:6], T.ki[:, 0:2], 4, None, A.logical_shift_right, None, ["ip"], ["gci"])
-    cp(T.sgl[:, :], T.ki[:, 0:2], ["ip"], ["sgl"])
     cp(T.kf[:, 0:2], T.ki[:, 2:4], ["kci"], ["kcf"])
-    cp(T.kf[:, 2:4], T.ki[:, 4:6], ["gci"], ["gcf"])
     tsc(T.kf[:, 4:6], T.ki[:, 2:4], 0.5, None, A.add, None, ["kci"], ["khf"])
-    k16, g16, k05 = T.kf[:, 0:1], T.kf[:, 2:3], T.kf[:, 4:5]
+    cp(T.kf[:, 2:4], T.ki[:, 4:6], ["gci"], ["gcf"])
     cp(T.eb[:, 3:515:4], T.idb[:, :], ["idb"], ["eb"])
-    act(T.nb[:, 3:515:4], T.idb[:, :], F.Copy, ["idb"], ["nb"], scale=-1.0)
-    for b in range(4):
-        quant("ep", 128 * b, 128 * b + 128, "eb", 3 - b, ["eb"], ["ep"])
+    fill(T.gb[:, :], 0.0, (), ["gb"])
+    fill(T.pb[:, :], 1.0, (), ["pb"])
+    k16, g16, k05 = T.kf[:, 0:1], T.kf[:, 2:3], T.kf[:, 4:5]
+    act(T.nb[:, :], T.eb[:, :], F.Copy, ["eb"], ["nb"], scale=-1.0)
+    act(T.pa[:, :], T.im16[:, :], F.Abs, ["im16", "kcf"], ["pa"], scale=-1.0, bias=k16)
+    act(T.pb[:, 0:512:4], T.pa[:, :], F.Relu, ["pa", "pb"], ["pb0"], scale=-128.0, bias=128.0)
+    act(T.pb[:, 2:512:4], T.im16[:, :], F.Copy, ["im16", "pb"], ["pb2"])
+    act(T.gb[0:1, 1:32:4], T.one[0:1, 0:8], F.Copy, ["one", "gb"], ["gb1"], scale=float(K * rank))
+    act(T.gb[0:1, 33:64:4], T.cf[0:1, 16:32:2], F.Copy, ["h16", "gb"], ["gb3"])
+    act(T.gb[0:1, 2:64:4], T.one[0:1, 0:16], F.Copy, ["one", "gb"], ["gb4"])
+    act(T.cf[:, 96:112], T.cf[:, 0:16], F.Abs, ["c8", "gcf"], ["away"], scale=-1.0, bias=g16)
+    act(T.cf[:, 32:48], T.cf[:, 96:112], F.Relu, ["away"], ["hm"], scale=-8.0, bias=8.0)
 
     tsc(T.li[:, 0:4], T.wr[:, 1:9:2], 7, None, A.logical_shift_right, None, ["wr"], ["h4i"])
     cp(T.lff[:, 0:4], T.li[:, 0:4], ["h4i"], ["h4f"])
 
-    def spread(dst, col, name, rd):
+    def spread(dst, col, name, rd, both):
         for b in range(4):
             x = T.lff[:, col + b:col + b + 1]
-            if b % 2:
+            if both and b % 2:
                 act(T[dst][:, 32 * b:32 * b + 32], T.one[:, 0:32], F.Copy, ["one", rd], [dst + ".%d" % b], scale=x)
             else:
                 tsc(T[dst][:, 32 * b:32 * b + 32], T.one[:, 0:32], x, None, A.mult, None, ["one", rd], [dst + ".%d" % b])
         turn(T[name][:, :], T[dst][:, :], [dst + ".%d" % b for b in range(4)], [name])
 
-    spread("ah", 0, "hd", "h4f")
+    spread("ah", 0, "hd", "h4f", False)
 
     def mask(h):
         tsc(T.mk[:, E * h:E * h + E], T.hd[:, :], float(h), None, A.is_equal, None, ["hd"], ["mk%d" % h])
@@ -285,16 +292,12 @@ def rank_program(g, core, T, topo):
             mask(h + 2)
         act(T.jk[:, s0:s1], T.cu[:, s0:s1], F.Sign, ["cu%d" % h, "khf"], ["jk%d" % h, "acc%d" % h], scale=-1.0, bias=k05, accum_out=T.lff[:, 16 + h:17 + h])
     quant("qmb", 0, 160, "mb", 0, ["mb"], ["qmb"])
+    cp(T.lff[:, 4:8], T.wr[:, 1:9:2], ["wr"], ["r4f"])
     tsc(T.ls[:, :], T.lff[:, 16:24], 0.5, 64.0, A.mult, A.add, ["acc%d" % h for h in range(N)], ["ls"])
     pick("mw0", 0, "qmb", 0, 128, "ls", 0, ["qmb"], ["qmb"], ["ls"], "mw0.m", "mw0.m_s")
 
-    def view(name, a, n, codes):
-        x = T[name][:, a:a + n]
-        return x.bitcast(u8) if codes else x
-
     def send(stage, src, rd):
-        t, codes = int(stage[1]), stage[0] != "l" and not stage.endswith("s")
-        tail = "_s" if stage.endswith("s") else ""
+        t, tail, codes, base = kind(stage)
         i = peers(T, topo, core).index(core)
         waits("g", rd, ())
         for part in calls(T, topo, core, stage):
@@ -303,9 +306,9 @@ def rank_program(g, core, T, topo):
                 if stage[0] == "l":
                     dst = T["rl%d" % t][:, rank:rank + 1] if x == d else T["rq%d" % t][:, i:i + 1]
                 elif x == d:
-                    dst = view("iw%d" % t + tail, K * rank + (E if stage[0] == "c" else 0), K, codes)
+                    dst = view(T, "iw%d" % t + tail, base + K * rank, K, codes)
                 else:
-                    dst = view("r" + stage[:2] + tail, K * i, K, codes)
+                    dst = view(T, "r" + stage[:2] + tail, K * i, K, codes)
                 rid, pid = topo.addr(x, core)
                 tr.append(RemoteDMATransfer(dst_ids=[DstId(rid=rid, pnc=pid)], dma_engine_mask=bits(e),
                                             remote_sem=T.sem[("a_" if x == d else "r_") + stage], src=src(T.rank_of(d)), dst=dst))
@@ -315,20 +318,17 @@ def rank_program(g, core, T, topo):
         return ("a_" + stage, count["a_" + stage])
 
     def columns(t, base, stage, rd):
-        m = "mw%d" % t
-        tc = send(stage, lambda h: view(m, base + K * h, K, True), [rd])
-        ts = send(stage + "s", lambda h: view(m + "_s", base + K * h, K, False), [rd + "_s"])
-        at = base + K * rank
-        dmas([("y", view("iw%d" % t, at, K, True), view(m, at, K, True)),
-              ("y", view("iw%d_s" % t, at, K, False), view(m + "_s", at, K, False))], "h" + stage, [rd, rd + "_s"], ["home"])
-        part = "iw%d" % t + (".c" if base else ".m")
-        wrote[part], wrote[part + "_s"] = [tc] + wrote["home"], [ts] + wrote["home"]
-        del wrote["home"]
+        m, at = "mw%d" % t, base + K * rank
+        tc = send(stage, lambda h: view(T, m, base + K * h, K, True), [rd])
+        ts = send(stage + "s", lambda h: view(T, m + "_s", base + K * h, K, False), [rd + "_s"])
+        dmas([("y", view(T, "iw%d" % t, at, K, True), view(T, m, at, K, True)),
+              ("y", view(T, "iw%d_s" % t, at, K, False), view(T, m + "_s", at, K, False))], "h" + stage, [rd, rd + "_s"], ["home"])
+        part, h = "iw%d" % t + (".c" if base else ".m"), wrote.pop("home")
+        wrote[part], wrote[part + "_s"] = [tc] + h, [ts] + h
 
     columns(0, 0, "m0", "mw0.m")
 
-    cp(T.lff[:, 4:8], T.wr[:, 1:9:2], ["wr"], ["r4f"])
-    spread("ar", 4, "rb", "r4f")
+    spread("ar", 4, "rb", "r4f", True)
     for b in range(4):
         act(T.js[:, 128 * b:128 * b + 128], T.rb[:, :], F.Sign, ["rb", "r4f"], ["js%d" % b, "sa%d" % b], scale=-1.0, bias=T.lff[:, 4 + b:5 + b], accum_out=T.lff[:, 8 + b:9 + b])
     cp(T.li[:, 8:16], T.ls[:, :], ["ls"], ["lsi"])
@@ -345,34 +345,23 @@ def rank_program(g, core, T, topo):
     cp(T.fd[:, 0:48:2], T.fk[:, :], ["fk"], ["fd0"])
     cp(T.fd[:, 1:48:2], T.fk[:, :], ["fk"], ["fd1"])
     tsc(T.lff[:, 12:16], T.lff[:, 8:12], 0.5, 63.5, A.mult, A.add, ["sa%d" % b for b in range(4)], ["s4"])
-    spread("asl", 12, "slb", "s4")
+    spread("asl", 12, "slb", "s4", False)
     for k in range(3):
+        o, i = T.dk[:, 256 * k:256 * k + 256], T.slb[:, :].indirect(T.fd[:, 16 * k:16 * k + 16])
+        if k == 1:
+            act(o, i, F.Copy, ["slb", "fd0", "fd1"], ["dk1"])
+        else:
+            cp(o, i, ["slb", "fd0", "fd1"], ["dk%d" % k])
+    for k in (0, 2, 1):
         d0, d1 = 256 * k, 256 * k + 256
-        cp(T.dk[:, d0:d1], T.slb[:, :].indirect(T.fd[:, 16 * k:16 * k + 16]), ["slb", "fd0", "fd1"], ["dk%d" % k])
         turn(T.dkt[:, d0:d1], T.dk[:, d0:d1], ["dk%d" % k], ["dkt%d" % k])
         cp(T.lf[:, 8 * k:8 * k + 8], T.dkt[:, d0:d1:32], ["dkt%d" % k], ["lf%d" % k])
     pick("bb", 0, "qmb", 128, 160, "lb", 0, ["qmb"], ["qmb"], ["lb"], "bb", "bb_s")
     for b in range(4):
-        quant("en", 128 * b, 128 * b + 128, "nb", 3 - b, ["nb"], ["en"])
+        quant("ep", 128 * b, 128 * b + 128, "eb", 3 - b, ["eb"], ["ep"])
+    act(T.lff[:, 48:52], T.uc[:, :], F.Copy, ["uc"], ["ucf"])
     for t in range(4):
-        tsc(T.ub[:, t:512:4], T.one[:, :], T.uc[:, t:t + 1], None, A.mult, None, ["one", "uc"], ["ub%d" % t])
-    quant("qu", 0, 128, "ub", 0, ["ub%d" % t for t in range(4)], ["qu"])
-
-    tsc(T.pb[:, 0:512:4], T.im16[:, :], k16, 128.0, A.is_equal, A.mult, ["im16", "kcf", "pb"], ["pb0"])
-    fill(T.pb[0:1, 1:512:4], 1.0, ["pb"], ["pb1"])
-    cp(T.pb[0:1, 2:512:4], T.im16[0:1, :], ["im16", "pb"], ["pb2"])
-    fill(T.pb[:, 3:512:4], 1.0, ["pb"], ["pb3"])
-    quant("pc", 0, 128, "pb", 0, ["pb0", "pb1", "pb2", "pb3"], ["pc"])
-    fill(T.gb[:, :], 0.0, (), ["gb"])
-    fill(T.gb2[:, :], 0.0, (), ["gb2"])
-    fill(T.gb[0:1, 1:32:4], float(K * rank), ["gb"], ["gb1"])
-    cp(T.gb[0:1, 33:64:4], T.cf[0:1, 16:32:2], ["h16", "gb"], ["gb3"])
-    fill(T.gb[0:1, 2:64:4], 1.0, ["gb"], ["gb4"])
-    tsc(T.cf[:, 32:48], T.cf[:, 0:16], g16, 8.0, A.is_equal, A.mult, ["c8", "gcf"], ["hm"])
-    tsc(T.cf[:, 48:64], T.im16[:, 0:16], k16, None, A.is_lt, None, ["im16", "kcf"], ["lt"])
-    tsc(T.cf[:, 64:80], T.cf[:, 48:64], -2.0 ** -24, 1.0, A.mult, A.add, ["lt"], ["mth"])
-    tsc(T.cf[:, 80:96], T.cf[:, 48:64], -2.0 ** -120, None, A.mult, None, ["lt"], ["bth"])
-    fill(T.sm[:, 4:5], 0.0, (), ["cnt0"])
+        act(T.ub[:, t:512:4], T.one[:, :], F.Copy, ["one", "ucf"], ["ub%d" % t], scale=T.lff[:, 48 + t:49 + t])
 
     def prefill_m(t):
         for b in range(4):
@@ -383,13 +372,6 @@ def rank_program(g, core, T, topo):
             mm("zb%d" % b, "ep", 128 * b, "bb", 0, True, False, ["ep", "bb", "bb_s"])
 
     prefill_b()
-    prefill_m(0)
-    cp(T.pob[:, :].indirect(T.ls[:, :]), T.ij[:, :], ["ls", "ij"], ["pob"])
-    tsc(T.dupl[:, :], T.cf[:, 16:32], k16, None, A.add, None, ["h16", "kcf"], ["dupl"])
-    cp(T.pd[:, :], T.pob[:, :].indirect(T.dupl[:, :]), ["pob", "dupl"], ["pd"])
-    turn(T.pdt[:, :], T.pd[:, :], ["pd"], ["pdt"])
-    cp(T.ln[:, :], T.pdt[:, 0:256:32], ["pdt"], ["ln"])
-    quant("qw", 0, 256, "wt", 0, ["wt"], ["qw"])
 
     for t in range(R):
         iw, mw, f, lst = "iw%d" % t, "mw%d" % t, "f%d" % t, "lst%d" % t
@@ -399,24 +381,36 @@ def rank_program(g, core, T, topo):
         for k in range(3):
             for b in range(4):
                 mm("zb%d" % b, "ep", 128 * b, f, 128 * k, False, k == 2, ["ep", f + ".%d" % k, f + "s.%d" % k])
+        if t == 0:
+            for b in range(4):
+                quant("en", 128 * b, 128 * b + 128, "nb", 3 - b, ["nb"], ["en"])
+            prefill_m(0)
         for b in range(4):
-            if b % 2 == 0:
+            if b % 2:
                 tsc(T.z[:, b:512:4], T["zb%d" % b][:, 0:128], 0.25, None, A.mult, None, ["zb%d" % b], ["z%d" % b])
             else:
                 act(T.z[:, b:512:4], T["zb%d" % b][:, 0:128], F.Copy, ["zb%d" % b], ["z%d" % b], scale=0.25)
         quant(mw, 128, 256, "z", 0, ["z%d" % b for b in range(4)], [mw + ".c", mw + ".c_s"])
         for b in range(4):
             mm("db%d" % b, "ep", 128 * b, mw, 128, False, True, ["ep", mw + ".c"])
+        if t == 0:
+            quant("qu", 0, 128, "ub", 0, ["ub%d" % b for b in range(4)], ["qu"])
+            quant("pc", 0, 128, "pb", 0, ["pb", "pb0", "pb2"], ["pc"])
         if not last:
             columns(t, E, "c%d" % t, mw + ".c")
         for b in range(4):
-            if b % 2 == 0:
+            if b % 2:
                 cp(T.dd[:, b:512:4], T["db%d" % b][:, 0:128], ["db%d" % b], ["dd%d" % b])
             else:
                 act(T.dd[:, b:512:4], T["db%d" % b][:, 0:128], F.Copy, ["db%d" % b], ["dd%d" % b])
         quant("qd", 0, 128, "dd", 0, ["dd%d" % b for b in range(4)], ["qd"])
         mm("zb1", "qu", 0, "qd", 0, True, True, ["qu", "qd"])
         mm("zb0", "qd", 0, "qu", 0, True, True, ["qu", "qd"])
+        if t == 0:
+            tsc(T.cf[:, 48:64], T.im16[:, 0:16], k16, None, A.is_lt, None, ["im16", "kcf"], ["lt"])
+            tsc(T.cf[:, 64:80], T.cf[:, 48:64], -2.0 ** -24, 1.0, A.mult, A.add, ["lt"], ["mth"])
+            tsc(T.cf[:, 80:96], T.cf[:, 48:64], -2.0 ** -120, None, A.mult, None, ["lt"], ["bth"])
+            cp(T.sgl[:, :], T.ki[:, 0:2], ["ip"], ["sgl"])
         act(T.sx[:, :], T.zb1[:, 0:128], F.Abs, ["zb1"], ["sx"])
         op("v", lambda: v.tensor_reduce(T.sm[:, 0:1], T.zb0[:, 0:2], AxisListType.X, A.max, apply_absolute_value=True), ["zb0"], ["sc"])
         tsc(T.tt[:, 0:16], T.cf[:, 64:80], T.sm[:, 0:1], None, A.mult, None, ["mth", "sc"], ["th0"])
@@ -426,6 +420,8 @@ def rank_program(g, core, T, topo):
         tsc(T.gb[:, 0:64:4], T.cf[:, 32:48], T.sm[:, 2:3], None, A.is_gt, None, ["hm", "rk", "gb"], ["gb0"])
         quant("qg", 0, 128, "gb", 0, ["gb0", "gb1", "gb3", "gb4"], ["qg"])
         mm("zb2", "pc", 0, "qg", 0, True, True, ["pc", "qg"])
+        if t == 0:
+            fill(T.sm[:, 4:5], 0.0, (), ["cnt0"])
         tsc(T.sm[:, 5 + t:6 + t], T.sm[:, 2:3], 8.0, T.sm[:, 4 + t:5 + t], A.is_lt, A.add, ["rk", "cnt%d" % t], ["cnt%d" % (t + 1)])
         cp(T[lst][:, :], T.zb2[:, 0:16], ["zb2"], [lst])
         if not last:
@@ -440,9 +436,16 @@ def rank_program(g, core, T, topo):
             mm("zb3", "pc", 0, "qg2", 0, True, True, ["pc", "qg2"])
         else:
             prefill_m(t + 1)
+        if t == 0:
+            cp(T.pob[:, :].indirect(T.ls[:, :]), T.ij[:, :], ["ls", "ij"], ["pob"])
+            tsc(T.dupl[:, :], T.cf[:, 16:32], k16, None, A.add, None, ["h16", "kcf"], ["dupl"])
+            cp(T.pd[:, :], T.pob[:, :].indirect(T.dupl[:, :]), ["pob", "dupl"], ["pd"])
+            turn(T.pdt[:, :], T.pd[:, :], ["pd"], ["pdt"])
+            cp(T.ln[:, :], T.pdt[:, 0:256:32], ["pdt"], ["ln"])
+            quant("qw", 0, 256, "wt", 0, ["wt"], ["qw"])
         pick(nt, 0, nw, 0, 128, "ln", 0, [nw + ".m"], [nw + ".m_s"], ["ln"], nt, nt + "_s")
         if last:
-            dmas([("y", T.oc[:, :], view(nt, 0, 128, True))], "st", [nt], ())
+            dmas([("y", T.oc[:, :], view(T, nt, 0, 128, True))], "st", [nt], ())
             act(T.ups[:, :], T.zb3[:, 0:128], F.Copy, ["zb3"], ["ups"])
             dmas([("y", T.osc[4 * k:4 * k + 4, :], T[nt + "_s"][32 * k:32 * k + 4, :]) for k in range(4)], "st", [nt + "_s"], ())
             cp(T.upn[:, :], T.ups[:, :].indirect(T.ln[:, :]), ["ups", "ln"], ["upn"])
@@ -451,6 +454,8 @@ def rank_program(g, core, T, topo):
             mm("zb%d" % o, "qw", 128 * o, nt, 0, True, True, ["qw", nt, nt + "_s"])
         act(T[ys][:, 0:128], T.zb0[:, 0:128], F.Copy, ["zb0"], [ys + ".0"])
         cp(T[ys][:, 128:256], T.zb1[:, 0:128], ["zb1"], [ys + ".1"])
+        if t == 0:
+            fill(T.gb2[:, :], 0.0, (), ["gb2"])
         if not last:
             prefill_b()
             dmas([("y", T.y[:, 256 * t:256 * t + 256], T[ys][:, :])], "st", [ys + ".0", ys + ".1"], ())

@@ -3,6 +3,7 @@ from concourse.mybir import dt, AluOpType as A, AxisListType, ActivationFunction
 
 N, V, E, R, O, K = 8, 32, 128, 3, 2, 16
 X4, U8, U16, BF, F32, I32 = "float8_e4m3fn_x4", "uint8", "uint16", "bfloat16", "float32", "int32"
+EPS = 2.0 ** -120
 SCRATCH = {}
 
 
@@ -14,26 +15,20 @@ for _i in range(4):
     _buf("zb%d" % _i, 512, F32, "psum")
     _buf("db%d" % _i, 512, F32, "psum")
 for _n, _c, _d in (
-        ("wr", 10, I32), ("mb", 640, BF), ("uc", 4, BF), ("wt", 1024, BF),
+        ("wr", 10, I32), ("mb", 672, BF), ("uc", 4, BF), ("wt", 1024, BF), ("pw", 512, BF),
         ("one", 128, BF), ("idb", 128, BF), ("eb", 516, BF), ("nb", 516, BF), ("pb", 512, BF), ("gb", 512, BF), ("gb2", 512, BF), ("ub", 512, BF),
-        ("im16", 128, F32), ("pa", 128, F32), ("ij", 128, BF),
-        ("ki", 8, I32),
-        ("kf", 8, F32),
-        ("cf", 112, F32),
-        ("li", 40, I32),
-        ("lff", 52, F32),
-        ("sm", 12, F32),
-        ("tt", 48, F32),
+        ("im16", 128, F32), ("pa", 128, F32), ("ij", 128, BF), ("ki", 8, I32), ("kf", 8, F32), ("cf", 112, F32), ("li", 40, I32), ("lff", 52, F32),
+        ("sm", 12, F32), ("tt", 48, F32),
         ("sgl", 2, U16), ("dupl", 16, U16), ("ls", 8, U16), ("lb", 8, U16), ("fd", 48, U16), ("lf", 24, U16), ("ln", 8, U16),
-        ("ah", 128, BF), ("hd", 128, BF), ("mk", 1024, BF), ("cu", 1024, BF), ("jk", 1024, BF),
+        ("ah", 128, BF), ("hd", 128, BF), ("mk", 128, BF), ("cu", 128, BF), ("jk", 128, BF), ("jb", 8, BF),
         ("ar", 128, F32), ("rb", 128, F32), ("js", 512, BF), ("asl", 128, BF), ("slb", 128, BF),
         ("ft", 24, F32), ("fk", 24, F32), ("dk", 768, BF), ("dkt", 768, BF),
-        ("pob", 128, BF), ("pd", 256, BF), ("pdt", 256, BF), ("ups", 128, F32), ("upn", 128, F32),
+        ("pob", 128, BF), ("pd", 256, BF), ("pdt", 256, BF), ("ups", 128, F32), ("pn", 128, BF),
         ("z", 512, BF), ("dd", 512, BF), ("sx", 128, F32)):
     _buf(_n, _c, _d)
-for _n, _c in (("qmb", 160), ("bb", 128), ("ep", 512), ("en", 512), ("pc", 128), ("qg", 128), ("qg2", 128), ("qu", 128), ("qw", 256), ("qd", 128),
+for _n, _c in (("qmb", 160), ("qx", 128), ("qp", 128), ("bb", 128), ("ep", 512), ("en", 512), ("pc", 128), ("qg", 128), ("qg2", 128), ("qu", 128), ("qw", 256), ("qd", 128),
                ("mw0", 256), ("mw1", 256), ("mw2", 256), ("mw3", 128), ("iw0", 256), ("iw1", 256), ("iw2", 128),
-               ("rm0", 32), ("rc0", 32), ("rc1", 32), ("f0", 384), ("f1", 384), ("f2", 384), ("nt0", 128), ("nt1", 128), ("nt2", 128)):
+               ("rm0", 32), ("rc0", 64), ("rc1", 64), ("f0", 384), ("f1", 384), ("f2", 384), ("nt0", 128), ("nt1", 128), ("nt2", 128)):
     _buf(_n, _c, X4)
     _buf(_n + "_s", _c, U8)
 for _t in range(R):
@@ -44,9 +39,9 @@ for _t in range(R - 1):
     _buf("rq%d" % _t, 2, U16)
 
 STAGES = ["m0", "m0s", "c0", "c0s", "l0", "c1", "c1s", "l1"]
-SEMAPHORES = ["qv", "qs", "qt", "qg", "ls", "ldr", "ldm", "ldu", "ldw", "hm0", "hc0", "hc1", "hl0", "hl1", "st"]
+SEMAPHORES = ["qv", "qs", "qt", "qg", "ls", "lf", "ldr", "ldm", "ldu", "ldw", "hm0", "hc0", "hc1", "hl0", "hl1", "st"]
 SEMAPHORES += ["a_" + s for s in STAGES] + ["r_" + s for s in STAGES]
-SPLIT = ("m0", "m0s", "l0", "l1")
+FAR, NEAR = 0, 1
 
 
 def direct(T, topo, c):
@@ -57,11 +52,24 @@ def cross(T, topo, c):
     return [d for d in T.cores if d != c and not topo.may_write(c, d)]
 
 
+def peers(T, topo, c):
+    return [x for x in topo.cores_of(c) if T.rank_of(x) is not None]
+
+
 def relay(T, topo, c, d):
     own = [x for x in topo.cores_of(c) if T.rank_of(x) is None and topo.may_write(x, d)]
     near = [x for x in own if topo.die(x) == topo.die(d)] or own
     same = [x for x in cross(T, topo, c) if topo.die(x) == topo.die(d)]
     return near[same.index(d) % len(near)]
+
+
+def chips(T, topo, c):
+    out = []
+    for d in cross(T, topo, c):
+        if not out or d not in topo.cores_of(out[-1][0]):
+            out.append([])
+        out[-1].append(d)
+    return out
 
 
 def pow2(n):
@@ -88,32 +96,50 @@ def share(topo, c, dsts):
     return out
 
 
-def calls(T, topo, c, stage):
-    near = [(d, d) for d in direct(T, topo, c)]
-    far = [(d, relay(T, topo, c, d)) for d in cross(T, topo, c)]
-    out = []
-    for part in ([far, near] if stage in SPLIT else [far + near]):
-        if part:
-            e = share(topo, c, [x for _, x in part])
-            out.append([(d, x, e[x]) for d, x in part])
-    return out
-
-
 def bits(engines):
     return sum(1 << e for e in engines)
 
 
-def peers(T, topo, c):
-    return [x for x in topo.cores_of(c) if T.rank_of(x) is not None]
+def kind(stage):
+    return int(stage[1]), "_s" if stage.endswith("s") else "", stage[0] != "l" and not stage.endswith("s"), E if stage[0] == "c" else 0
+
+
+def roads(T, topo, c, stage, way):
+    if way == NEAR:
+        out = [(d, [d]) for d in direct(T, topo, c)]
+    elif stage[0] == "c":
+        out = [(relay(T, topo, c, ds[(j + stage.endswith("s")) % len(ds)]), ds) for j, ds in enumerate(chips(T, topo, c))]
+    else:
+        out = [(relay(T, topo, c, d), [d]) for d in cross(T, topo, c)]
+    e = share(topo, c, [x for x, _ in out])
+    return [(x, e[x], ds) for x, ds in out]
+
+
+def onward(T, topo, x, stage):
+    mine = peers(T, topo, x)
+    ds = [r[2] for r in roads(T, topo, mine[0], stage, FAR) if r[0] == x] if mine else []
+    if not ds:
+        return []
+    ds = ds[0]
+    if len(ds) == 1:
+        return [(ds[0], topo.engines(x, ds[0]), 0, len(mine), mine[0])]
+    e = topo.engines(x, ds[0])
+    per = pow2(len(e) // (len(mine) * len(ds)))
+    out = []
+    for i, s in enumerate(mine):
+        for j, d in enumerate(ds):
+            k = len(out)
+            out.append((d, e[per * k:per * k + per], i * len(ds) + j, 1, s))
+    return out
 
 
 def landed(T, topo, c, stage):
     n = 0
     for s in T.cores:
         if s != c:
-            n += sum(len(e) for part in calls(T, topo, s, stage) for _, x, e in part if x == c)
-            if T.rank_of(c) is not None and not topo.may_write(s, c) and s == peers(T, topo, s)[0]:
-                n += len(topo.engines(relay(T, topo, s, c), c))
+            n += sum(len(e) for way in (FAR, NEAR) for x, e, _ in roads(T, topo, s, stage, way) if x == c)
+        if T.rank_of(c) is not None and s == peers(T, topo, s)[0] and not topo.may_write(s, c):
+            n += sum(len(o[1]) for x in topo.cores_of(s) if T.rank_of(x) is None for o in onward(T, topo, x, stage) if o[0] == c)
     return n
 
 
@@ -122,27 +148,27 @@ def view(T, name, a, n, codes):
     return x.bitcast(dt.uint8) if codes else x
 
 
-def kind(stage):
-    return int(stage[1]), "_s" if stage.endswith("s") else "", stage[0] != "l" and not stage.endswith("s"), E if stage[0] == "c" else 0
-
-
 def relay_program(g, core, T, topo):
-    mine = peers(T, topo, core)
-    todo = [d for d in cross(T, topo, mine[0]) if relay(T, topo, mine[0], d) == core]
-    if not todo:
-        return
-    d = todo[0]
-    rid, pid = topo.addr(d, core)
-    r0, n, e = T.rank_of(mine[0]), len(mine), topo.engines(core, d)
+    total = 0
     for st in STAGES:
+        out = onward(T, topo, core, st)
+        if not out:
+            continue
         t, tail, codes, base = kind(st)
-        if st[0] == "l":
-            src, dst = T["rq%d" % t][:, 0:n], T["rl%d" % t][:, r0:r0 + n]
-        else:
-            src, dst = view(T, "r" + st[:2] + tail, 0, K * n, codes), view(T, "iw%d" % t + tail, base + K * r0, K * n, codes)
+        tr = []
+        for d, e, a, n, s in out:
+            r = T.rank_of(s)
+            if st[0] == "l":
+                src, dst = T["rq%d" % t][:, a:a + n], T["rl%d" % t][:, r:r + n]
+            else:
+                src, dst = view(T, "r" + st[:2] + tail, K * a, K * n, codes), view(T, "iw%d" % t + tail, base + K * r, K * n, codes)
+            rid, pid = topo.addr(d, core)
+            tr.append(RemoteDMATransfer(dst_ids=[DstId(rid=rid, pnc=pid)], dma_engine_mask=bits(e), remote_sem=T.sem["a_" + st], src=src, dst=dst))
+            total += len(e)
         g.wait_ge(T.sem["r_" + st], landed(T, topo, core, st))
-        g.remote_dma(dst, src, T.sem["a_" + st], T.sem["ls"], pid, rid, bits(e))
-    g.wait_ge(T.sem["ls"], len(STAGES) * len(e))
+        g.remote_dma_fused(tr, local_sem=T.sem["ls"])
+    if total:
+        g.wait_ge(T.sem["ls"], total)
 
 
 def rank_program(g, core, T, topo):
@@ -216,8 +242,8 @@ def rank_program(g, core, T, topo):
     def act(o, i, fn, rd, wr, **kw):
         op("s", lambda: sc.activation(o, i, fn, **kw), rd, wr)
 
-    def iota(o, pattern, ch, wr):
-        op("g", lambda: g.iota(o, pattern, 0, ch, allow_small_or_imprecise_dtypes=True), (), [wr])
+    def iota(o, pattern, ch, wr, base=0):
+        op("g", lambda: g.iota(o, pattern, base, ch, allow_small_or_imprecise_dtypes=True), (), [wr])
 
     def quant(name, a, b, tile, x, rd, wr):
         op("v", lambda: v.quantize_mx(T[name][:, a:b], T[name + "_s"][:, a:b], T[tile][:, x:x + 4 * (b - a)]), rd, wr)
@@ -241,30 +267,27 @@ def rank_program(g, core, T, topo):
 
     fill(T.one[:, :], 1.0, (), ["one"])
     op("g", lambda: g.iota(T.ki[:, 0:2], [[0, 2]], 0, 1), (), ["ip"])
-    op("g", lambda: g.affine_select(T.idb[:, :], T.one[:, :], [[-1, 128]], A.is_equal, 0.0, 0, 1), ["one"], ["idb"])
     iota(T.im16[:, :], [[0, 8], [1, 16]], 0, "im16")
     iota(T.cf[:, 0:16], [[0, 2], [1, 8]], 0, "c8")
-    iota(T.cf[:, 16:32], [[16, 8], [0, 2]], 0, "h16")
-    iota(T.ij[:, :], [[1, 128]], 0, "ij")
-    fill(T.eb[:, :], 0.0, (), ["eb"])
+    iota(T.mb[:, 640:672], [[0, 32]], 0, "xz")
+    iota(T.pb[:, :], [[0, 512]], 0, "pb", 1)
+    op("g", lambda: g.affine_select(T.eb[:, 0:512], T.pb[:, :], [[-1, 512]], A.is_equal, 0.0, 3, 4), ["pb"], ["eb0"])
+    iota(T.eb[:, 512:516], [[0, 4]], 0, "eb1")
     tsc(T.ki[:, 2:4], T.ki[:, 0:2], 15, None, A.bitwise_and, None, ["ip"], ["kci"])
     tsc(T.ki[:, 4:6], T.ki[:, 0:2], 4, None, A.logical_shift_right, None, ["ip"], ["gci"])
     cp(T.kf[:, 0:2], T.ki[:, 2:4], ["kci"], ["kcf"])
+    fill(T.pw[:, :], 0.0, (), ["pw"])
     tsc(T.kf[:, 4:6], T.ki[:, 2:4], 0.5, None, A.add, None, ["kci"], ["khf"])
     cp(T.kf[:, 2:4], T.ki[:, 4:6], ["gci"], ["gcf"])
-    cp(T.eb[:, 3:515:4], T.idb[:, :], ["idb"], ["eb"])
-    fill(T.gb[:, :], 0.0, (), ["gb"])
-    fill(T.pb[:, :], 1.0, (), ["pb"])
     k16, g16, k05 = T.kf[:, 0:1], T.kf[:, 2:3], T.kf[:, 4:5]
-    act(T.nb[:, :], T.eb[:, :], F.Copy, ["eb"], ["nb"], scale=-1.0)
     act(T.pa[:, :], T.im16[:, :], F.Abs, ["im16", "kcf"], ["pa"], scale=-1.0, bias=k16)
-    act(T.pb[:, 0:512:4], T.pa[:, :], F.Relu, ["pa", "pb"], ["pb0"], scale=-128.0, bias=128.0)
-    act(T.pb[:, 2:512:4], T.im16[:, :], F.Copy, ["im16", "pb"], ["pb2"])
-    act(T.gb[0:1, 1:32:4], T.one[0:1, 0:8], F.Copy, ["one", "gb"], ["gb1"], scale=float(K * rank))
-    act(T.gb[0:1, 33:64:4], T.cf[0:1, 16:32:2], F.Copy, ["h16", "gb"], ["gb3"])
-    act(T.gb[0:1, 2:64:4], T.one[0:1, 0:16], F.Copy, ["one", "gb"], ["gb4"])
+    for i, c in enumerate((0.5, 8.0)):
+        act(T.pw[:, i:512:4], T.pa[:, :], F.Relu, ["pa", "pw"], ["pw%d" % i], scale=-c, bias=c)
+    act(T.cf[:, 48:64], T.im16[:, 0:16], F.Relu, ["im16", "kcf"], ["below"], scale=-1.0, bias=k16)
     act(T.cf[:, 96:112], T.cf[:, 0:16], F.Abs, ["c8", "gcf"], ["away"], scale=-1.0, bias=g16)
+    act(T.cf[:, 80:96], T.cf[:, 48:64], F.Sign, ["below"], ["lt"])
     act(T.cf[:, 32:48], T.cf[:, 96:112], F.Relu, ["away"], ["hm"], scale=-8.0, bias=8.0)
+    act(T.cf[:, 64:80], T.cf[:, 80:96], F.Copy, ["lt"], ["mth"], scale=-2.0 ** -24, bias=1.0)
 
     tsc(T.li[:, 0:4], T.wr[:, 1:9:2], 7, None, A.logical_shift_right, None, ["wr"], ["h4i"])
     cp(T.lff[:, 0:4], T.li[:, 0:4], ["h4i"], ["h4f"])
@@ -279,112 +302,135 @@ def rank_program(g, core, T, topo):
         turn(T[name][:, :], T[dst][:, :], [dst + ".%d" % b for b in range(4)], [name])
 
     spread("ah", 0, "hd", "h4f", False)
-
-    def mask(h):
-        tsc(T.mk[:, E * h:E * h + E], T.hd[:, :], float(h), None, A.is_equal, None, ["hd"], ["mk%d" % h])
-
-    mask(0)
-    mask(1)
-    for h in range(N):
-        s0, s1 = E * h, E * h + E
-        op("v", lambda: v.tensor_tensor_scan(T.cu[:, s0:s1], T.mk[:, s0:s1], T.mk[:, s0:s1], 0.0, A.add, A.max), ["mk%d" % h], ["cu%d" % h])
-        if h + 2 < N:
-            mask(h + 2)
-        act(T.jk[:, s0:s1], T.cu[:, s0:s1], F.Sign, ["cu%d" % h, "khf"], ["jk%d" % h, "acc%d" % h], scale=-1.0, bias=k05, accum_out=T.lff[:, 16 + h:17 + h])
+    tsc(T.mk[:, :], T.hd[:, :], g16, None, A.is_equal, None, ["hd", "gcf"], ["mk"])
+    op("v", lambda: v.tensor_tensor_scan(T.cu[:, :], T.mk[:, :], T.mk[:, :], 0.0, A.add, A.max), ["mk"], ["cu"])
+    act(T.jb[:, :], T.cu[:, 15:128:16], F.Sign, ["cu", "khf"], ["jb", "acc1"], scale=-1.0, bias=k05, accum_out=T.lff[:, 17:18])
+    act(T.jk[:, :], T.cu[:, :], F.Sign, ["cu", "khf"], ["jk", "acc0"], scale=-1.0, bias=k05, accum_out=T.lff[:, 16:17])
+    quant("qp", 0, 128, "pw", 0, ["pw", "pw0", "pw1"], ["qp"])
     quant("qmb", 0, 160, "mb", 0, ["mb"], ["qmb"])
-    cp(T.lff[:, 4:8], T.wr[:, 1:9:2], ["wr"], ["r4f"])
-    tsc(T.ls[:, :], T.lff[:, 16:24], 0.5, 64.0, A.mult, A.add, ["acc%d" % h for h in range(N)], ["ls"])
+    tsc(T.mb[:, 641:672:4], T.cf[:, 0:8], g16, T.lff[:, 17:18], A.is_equal, A.mult, ["c8", "gcf", "acc1", "xz"], ["x1"])
+    tsc(T.lff[:, 18:19], T.lff[:, 17:18], -16.0, T.lff[:, 16:17], A.mult, A.add, ["acc0", "acc1"], ["low"])
+    tsc(T.mb[:, 640:672:4], T.cf[:, 0:8], g16, T.lff[:, 18:19], A.is_equal, A.mult, ["c8", "gcf", "low", "xz"], ["x0"])
+    quant("qx", 0, 128, "mb", 160, ["mb", "xz", "x0", "x1"], ["qx"])
+    mm("db0", "qp", 0, "qx", 0, True, True, ["qp", "qx"])
+    tsc(T.ls[:, :], T.db0[:, 120:128], 64.0, None, A.add, None, ["db0"], ["ls"])
     pick("mw0", 0, "qmb", 0, 128, "ls", 0, ["qmb"], ["qmb"], ["ls"], "mw0.m", "mw0.m_s")
+    cp(T.lff[:, 4:8], T.wr[:, 1:9:2], ["wr"], ["r4f"])
 
-    def send(stage, src, rd):
+    def send(stage, way, src, rd, local="ls"):
         t, tail, codes, base = kind(stage)
         i = peers(T, topo, core).index(core)
         waits("g", rd, ())
-        for part in calls(T, topo, core, stage):
-            tr = []
-            for d, x, e in part:
-                if stage[0] == "l":
-                    dst = T["rl%d" % t][:, rank:rank + 1] if x == d else T["rq%d" % t][:, i:i + 1]
-                elif x == d:
-                    dst = view(T, "iw%d" % t + tail, base + K * rank, K, codes)
-                else:
-                    dst = view(T, "r" + stage[:2] + tail, K * i, K, codes)
-                rid, pid = topo.addr(x, core)
-                tr.append(RemoteDMATransfer(dst_ids=[DstId(rid=rid, pnc=pid)], dma_engine_mask=bits(e),
-                                            remote_sem=T.sem[("a_" if x == d else "r_") + stage], src=src(T.rank_of(d)), dst=dst))
-                count["ls"] = count.get("ls", 0) + len(e)
-            g.remote_dma_fused(tr, local_sem=T.sem["ls"])
+        tr = []
+        for x, e, ds in roads(T, topo, core, stage, way):
+            n = len(ds)
+            if stage[0] == "l":
+                dst = T["rl%d" % t][:, rank:rank + 1] if way == NEAR else T["rq%d" % t][:, i:i + 1]
+            elif way == NEAR:
+                dst = view(T, "iw%d" % t + tail, base + K * rank, K, codes)
+            else:
+                dst = view(T, "r" + stage[:2] + tail, K * n * i, K * n, codes)
+            rid, pid = topo.addr(x, core)
+            tr.append(RemoteDMATransfer(dst_ids=[DstId(rid=rid, pnc=pid)], dma_engine_mask=bits(e),
+                                        remote_sem=T.sem[("a_" if way == NEAR else "r_") + stage], src=src(T.rank_of(ds[0]), n), dst=dst))
+            count[local] = count.get(local, 0) + len(e)
+        g.remote_dma_fused(tr, local_sem=T.sem[local])
         count["a_" + stage] = landed(T, topo, core, stage)
-        return ("a_" + stage, count["a_" + stage])
 
-    def columns(t, base, stage, rd):
-        m, at = "mw%d" % t, base + K * rank
-        tc = send(stage, lambda h: view(T, m, base + K * h, K, True), [rd])
-        ts = send(stage + "s", lambda h: view(T, m + "_s", base + K * h, K, False), [rd + "_s"])
-        dmas([("y", view(T, "iw%d" % t, at, K, True), view(T, m, at, K, True)),
-              ("y", view(T, "iw%d_s" % t, at, K, False), view(T, m + "_s", at, K, False))], "h" + stage, [rd, rd + "_s"], ["home"])
-        part, h = "iw%d" % t + (".c" if base else ".m"), wrote.pop("home")
-        wrote[part], wrote[part + "_s"] = [tc] + h, [ts] + h
+    def columns(stage, way, local="ls"):
+        t, tail, codes, base = kind(stage)
+        m = "mw%d" % t
+        send(stage, way, lambda h, n: view(T, m + tail, base + K * h, K * n, codes), [m + (".c" if base else ".m") + tail], local)
 
-    columns(0, 0, "m0", "mw0.m")
+    def home(stage, after):
+        t, _, _, base = kind(stage)
+        m, iw, part, at = "mw%d" % t, "iw%d" % t, ".c" if base else ".m", base + K * rank
+        dmas([("y", view(T, iw, at, K, True), view(T, m, at, K, True)),
+              ("y", view(T, iw + "_s", at, K, False), view(T, m + "_s", at, K, False))], "h" + stage, [m + part, m + part + "_s"] + after, ["home"])
+        h = wrote.pop("home")
+        for x, y in (("", ""), ("s", "_s")):
+            wrote[iw + part + y] = [("a_" + stage + x, count["a_" + stage + x])] + h
+
+    for way, local in ((FAR, "lf"), (NEAR, "ls")):
+        for st in ("m0", "m0s"):
+            columns(st, way, local)
+    wrote["left"] = [("lf", count["lf"])]
+    home("m0", ["left"])
+    op("g", lambda: g.affine_select(T.idb[:, :], T.one[:, :], [[-1, 128]], A.is_equal, 0.0, 0, 1), ["one"], ["idb"])
+    iota(T.cf[:, 16:32], [[16, 8], [0, 2]], 0, "h16")
+    iota(T.gb[:, :], [[0, 512]], 0, "gb")
+    iota(T.ij[:, :], [[1, 128]], 0, "ij")
+    iota(T.gb2[:, :], [[0, 512]], 0, "gb2")
 
     spread("ar", 4, "rb", "r4f", True)
     for b in range(4):
         act(T.js[:, 128 * b:128 * b + 128], T.rb[:, :], F.Sign, ["rb", "r4f"], ["js%d" % b, "sa%d" % b], scale=-1.0, bias=T.lff[:, 4 + b:5 + b], accum_out=T.lff[:, 8 + b:9 + b])
+    act(T.pb[:, 0:512:4], T.pa[:, :], F.Relu, ["pa", "pb", "eb0"], ["pb0"], scale=-128.0, bias=128.0)
+    act(T.pb[:, 2:512:4], T.im16[:, :], F.Copy, ["im16", "pb", "eb0"], ["pb2"])
     cp(T.li[:, 8:16], T.ls[:, :], ["ls"], ["lsi"])
     tsc(T.li[:, 16:24], T.li[:, 8:16], 3, None, A.bitwise_and, None, ["lsi"], ["lqi"])
     tsc(T.li[:, 24:32], T.li[:, 8:16], 124, None, A.bitwise_and, None, ["lsi"], ["l4i"])
     tsc(T.li[:, 32:40], T.li[:, 8:16], 2, None, A.logical_shift_right, None, ["lsi"], ["lbi"])
-    cp(T.lff[:, 32:40], T.li[:, 16:24], ["lqi"], ["lqf"])
-    cp(T.lff[:, 40:48], T.li[:, 24:32], ["l4i"], ["lbf"])
+    for k in range(3):
+        tsc(T.ft[:, 8 * k:8 * k + 8], T.li[:, 16:24], float(k), float(k), A.is_le, A.add, ["lqi"], ["ft%d" % k])
+    for k in range(3):
+        ttn(T.fk[:, 8 * k:8 * k + 8], T.ft[:, 8 * k:8 * k + 8], T.li[:, 24:32], A.add, ["ft%d" % k, "l4i"], ["fk%d" % k])
     cp(T.lb[:, :], T.li[:, 32:40], ["lbi"], ["lb"])
-    for k in range(3):
-        tsc(T.ft[:, 8 * k:8 * k + 8], T.lff[:, 32:40], float(k), float(k), A.is_le, A.add, ["lqf"], ["ft%d" % k])
-    for k in range(3):
-        ttn(T.fk[:, 8 * k:8 * k + 8], T.ft[:, 8 * k:8 * k + 8], T.lff[:, 40:48], A.add, ["ft%d" % k, "lbf"], ["fk"])
-    cp(T.fd[:, 0:48:2], T.fk[:, :], ["fk"], ["fd0"])
-    cp(T.fd[:, 1:48:2], T.fk[:, :], ["fk"], ["fd1"])
+    cp(T.fd[:, 0:48:2], T.fk[:, :], ["fk0", "fk1", "fk2"], ["fd0"])
+    cp(T.fd[:, 1:48:2], T.fk[:, :], ["fk0", "fk1", "fk2"], ["fd1"])
     tsc(T.lff[:, 12:16], T.lff[:, 8:12], 0.5, 63.5, A.mult, A.add, ["sa%d" % b for b in range(4)], ["s4"])
-    spread("asl", 12, "slb", "s4", False)
+    spread("asl", 12, "slb", "s4", True)
     for k in range(3):
         o, i = T.dk[:, 256 * k:256 * k + 256], T.slb[:, :].indirect(T.fd[:, 16 * k:16 * k + 16])
-        if k == 1:
-            act(o, i, F.Copy, ["slb", "fd0", "fd1"], ["dk1"])
+        if k:
+            act(o, i, F.Copy, ["slb", "fd0", "fd1"], ["dk%d" % k])
         else:
             cp(o, i, ["slb", "fd0", "fd1"], ["dk%d" % k])
-    for k in (0, 2, 1):
+    for k in range(3):
         d0, d1 = 256 * k, 256 * k + 256
         turn(T.dkt[:, d0:d1], T.dk[:, d0:d1], ["dk%d" % k], ["dkt%d" % k])
         cp(T.lf[:, 8 * k:8 * k + 8], T.dkt[:, d0:d1:32], ["dkt%d" % k], ["lf%d" % k])
     pick("bb", 0, "qmb", 128, 160, "lb", 0, ["qmb"], ["qmb"], ["lb"], "bb", "bb_s")
     for b in range(4):
-        quant("ep", 128 * b, 128 * b + 128, "eb", 3 - b, ["eb"], ["ep"])
+        quant("ep", 128 * b, 128 * b + 128, "eb", 3 - b, ["eb0", "eb1"], ["ep%d" % b])
+    act(T.nb[:, :], T.eb[:, :], F.Copy, ["eb0", "eb1"], ["nb"], scale=-1.0)
     act(T.lff[:, 48:52], T.uc[:, :], F.Copy, ["uc"], ["ucf"])
-    for t in range(4):
+
+    def tile_u(t):
         act(T.ub[:, t:512:4], T.one[:, :], F.Copy, ["one", "ucf"], ["ub%d" % t], scale=T.lff[:, 48 + t:49 + t])
+
+    tile_u(0)
 
     def prefill_m(t):
         for b in range(4):
-            mm("db%d" % b, "en", 128 * b, "mw%d" % t, 0, True, False, ["en", "mw%d.m" % t, "mw%d.m_s" % t])
+            mm("db%d" % b, "en", 128 * b, "mw%d" % t, 0, True, False, ["en%d" % b, "mw%d.m" % t, "mw%d.m_s" % t])
 
     def prefill_b():
         for b in range(4):
-            mm("zb%d" % b, "ep", 128 * b, "bb", 0, True, False, ["ep", "bb", "bb_s"])
+            mm("zb%d" % b, "ep", 128 * b, "bb", 0, True, False, ["ep%d" % b, "bb", "bb_s"])
 
     prefill_b()
 
     for t in range(R):
         iw, mw, f, lst = "iw%d" % t, "mw%d" % t, "f%d" % t, "lst%d" % t
-        nw, nt, ys, last = "mw%d" % (t + 1), "nt%d" % t, "ys%d" % t, t == R - 1
+        nw, last = "mw%d" % (t + 1), t == R - 1
         for k in range(3):
             pick(f, 128 * k, iw, 0, 128, "lf", 8 * k, [iw + ".m"], [iw + ".m_s"], ["lf%d" % k], f + ".%d" % k, f + "s.%d" % k)
         for k in range(3):
             for b in range(4):
-                mm("zb%d" % b, "ep", 128 * b, f, 128 * k, False, k == 2, ["ep", f + ".%d" % k, f + "s.%d" % k])
+                mm("zb%d" % b, "ep", 128 * b, f, 128 * k, False, k == 2, ["ep%d" % b, f + ".%d" % k, f + "s.%d" % k])
         if t == 0:
             for b in range(4):
-                quant("en", 128 * b, 128 * b + 128, "nb", 3 - b, ["nb"], ["en"])
+                quant("en", 128 * b, 128 * b + 128, "nb", 3 - b, ["nb"], ["en%d" % b])
             prefill_m(0)
+            cp(T.sgl[:, :], T.ki[:, 0:2], ["ip"], ["sgl"])
+            for b in range(1, 4):
+                tile_u(b)
+        if t == 1:
+            turn(T.pdt[:, :], T.pd[:, :], ["pd"], ["pdt"])
+            quant("qw", 0, 256, "wt", 0, ["wt"], ["qw"])
+            cp(T.ln[:, :], T.pdt[:, 0:256:32], ["pdt"], ["ln"])
+            act(T.pn[:, :], T.idb[:, :].indirect(T.ln[:, :]), F.Copy, ["idb", "ln"], ["pn"])
         for b in range(4):
             if b % 2:
                 tsc(T.z[:, b:512:4], T["zb%d" % b][:, 0:128], 0.25, None, A.mult, None, ["zb%d" % b], ["z%d" % b])
@@ -392,77 +438,78 @@ def rank_program(g, core, T, topo):
                 act(T.z[:, b:512:4], T["zb%d" % b][:, 0:128], F.Copy, ["zb%d" % b], ["z%d" % b], scale=0.25)
         quant(mw, 128, 256, "z", 0, ["z%d" % b for b in range(4)], [mw + ".c", mw + ".c_s"])
         for b in range(4):
-            mm("db%d" % b, "ep", 128 * b, mw, 128, False, True, ["ep", mw + ".c"])
+            mm("db%d" % b, "ep", 128 * b, mw, 128, False, True, ["ep%d" % b, mw + ".c"])
         if t == 0:
             quant("qu", 0, 128, "ub", 0, ["ub%d" % b for b in range(4)], ["qu"])
             quant("pc", 0, 128, "pb", 0, ["pb", "pb0", "pb2"], ["pc"])
+            act(T.gb[0:1, 1:32:4], T.one[0:1, 0:8], F.Copy, ["one", "gb"], ["gb1"], scale=float(K * rank))
+            act(T.gb[0:1, 33:64:4], T.cf[0:1, 16:32:2], F.Copy, ["h16", "gb"], ["gb3"])
+            act(T.gb[0:1, 2:64:4], T.one[0:1, 0:16], F.Copy, ["one", "gb"], ["gb4"])
         if not last:
-            columns(t, E, "c%d" % t, mw + ".c")
+            for way in (FAR, NEAR):
+                for x in ("c%d", "c%ds"):
+                    columns(x % t, way)
         for b in range(4):
             if b % 2:
                 cp(T.dd[:, b:512:4], T["db%d" % b][:, 0:128], ["db%d" % b], ["dd%d" % b])
             else:
                 act(T.dd[:, b:512:4], T["db%d" % b][:, 0:128], F.Copy, ["db%d" % b], ["dd%d" % b])
         quant("qd", 0, 128, "dd", 0, ["dd%d" % b for b in range(4)], ["qd"])
-        mm("zb1", "qu", 0, "qd", 0, True, True, ["qu", "qd"])
         mm("zb0", "qd", 0, "qu", 0, True, True, ["qu", "qd"])
-        if t == 0:
-            tsc(T.cf[:, 48:64], T.im16[:, 0:16], k16, None, A.is_lt, None, ["im16", "kcf"], ["lt"])
-            tsc(T.cf[:, 64:80], T.cf[:, 48:64], -2.0 ** -24, 1.0, A.mult, A.add, ["lt"], ["mth"])
-            tsc(T.cf[:, 80:96], T.cf[:, 48:64], -2.0 ** -120, None, A.mult, None, ["lt"], ["bth"])
-            cp(T.sgl[:, :], T.ki[:, 0:2], ["ip"], ["sgl"])
-        act(T.sx[:, :], T.zb1[:, 0:128], F.Abs, ["zb1"], ["sx"])
-        op("v", lambda: v.tensor_reduce(T.sm[:, 0:1], T.zb0[:, 0:2], AxisListType.X, A.max, apply_absolute_value=True), ["zb0"], ["sc"])
-        tsc(T.tt[:, 0:16], T.cf[:, 64:80], T.sm[:, 0:1], None, A.mult, None, ["mth", "sc"], ["th0"])
-        ttn(T.tt[:, 16:32], T.tt[:, 0:16], T.cf[:, 80:96], A.add, ["th0", "bth"], ["th"])
+        mm("zb1", "qu", 0, "qd", 0, True, True, ["qu", "qd"])
+        act(T.sm[:, 0:1], T.zb0[:, 0:1], F.Abs, ["zb0"], ["sc"], bias=EPS)
+        act(T.sx[:, :], T.zb1[:, 0:128], F.Abs, ["zb1"], ["sx"], bias=EPS)
+        tsc(T.tt[:, 16:32], T.cf[:, 64:80], T.sm[:, 0:1], None, A.mult, None, ["mth", "sc"], ["th"])
         ttn(T.tt[:, 32:48], T.sx[:, :].indirect(T.sgl[:, 0:1]), T.tt[:, 16:32], A.is_gt, ["sx", "sgl", "th"], ["kk"])
         op("v", lambda: v.tensor_reduce(T.sm[:, 2:3], T.tt[:, 32:48], AxisListType.X, A.add), ["kk"], ["rk"])
         tsc(T.gb[:, 0:64:4], T.cf[:, 32:48], T.sm[:, 2:3], None, A.is_gt, None, ["hm", "rk", "gb"], ["gb0"])
         quant("qg", 0, 128, "gb", 0, ["gb0", "gb1", "gb3", "gb4"], ["qg"])
         mm("zb2", "pc", 0, "qg", 0, True, True, ["pc", "qg"])
         if t == 0:
-            fill(T.sm[:, 4:5], 0.0, (), ["cnt0"])
-        tsc(T.sm[:, 5 + t:6 + t], T.sm[:, 2:3], 8.0, T.sm[:, 4 + t:5 + t], A.is_lt, A.add, ["rk", "cnt%d" % t], ["cnt%d" % (t + 1)])
+            tsc(T.sm[:, 5:6], T.sm[:, 2:3], 8.0, None, A.is_lt, None, ["rk"], ["cnt1"])
+        else:
+            tsc(T.sm[:, 5 + t:6 + t], T.sm[:, 2:3], 8.0, T.sm[:, 4 + t:5 + t], A.is_lt, A.add, ["rk", "cnt%d" % t], ["cnt%d" % (t + 1)])
         cp(T[lst][:, :], T.zb2[:, 0:16], ["zb2"], [lst])
         if not last:
-            tl = send("l%d" % t, lambda h: T[lst][:, h:h + 1], [lst])
+            for way in (FAR, NEAR):
+                send("l%d" % t, way, lambda h, n: T[lst][:, h:h + n], [lst])
             dmas([("y", T["rl%d" % t][:, rank:rank + 1], T[lst][:, rank:rank + 1])], "hl%d" % t, [lst], ["home"])
-            wrote["rl%d" % t] = [tl] + wrote.pop("home")
+            wrote["rl%d" % t] = [("a_l%d" % t, count["a_l%d" % t])] + wrote.pop("home")
+            home("c%d" % t, [lst])
         else:
-            act(T.gb2[:, 3:512:4], T.idb[:, :], F.Copy, ["idb", "gb2", "cnt%d" % R], ["gb2d"], scale=T.sm[:, 4 + R:5 + R])
+            act(T.gb2[:, 3:512:4], T.pn[:, :], F.Copy, ["pn", "gb2", "cnt%d" % R], ["gb2d"], scale=T.sm[:, 4 + R:5 + R])
         pick(nw, 0, mw, 0, 256, lst, 8, [mw + ".m", mw + ".c"], [mw + ".m_s", mw + ".c_s"], [lst], nw + ".m", nw + ".m_s")
-        if last:
-            quant("qg2", 0, 128, "gb2", 0, ["gb2d"], ["qg2"])
-            mm("zb3", "pc", 0, "qg2", 0, True, True, ["pc", "qg2"])
-        else:
+        if not last:
             prefill_m(t + 1)
         if t == 0:
             cp(T.pob[:, :].indirect(T.ls[:, :]), T.ij[:, :], ["ls", "ij"], ["pob"])
             tsc(T.dupl[:, :], T.cf[:, 16:32], k16, None, A.add, None, ["h16", "kcf"], ["dupl"])
-            cp(T.pd[:, :], T.pob[:, :].indirect(T.dupl[:, :]), ["pob", "dupl"], ["pd"])
-            turn(T.pdt[:, :], T.pd[:, :], ["pd"], ["pdt"])
-            cp(T.ln[:, :], T.pdt[:, 0:256:32], ["pdt"], ["ln"])
-            quant("qw", 0, 256, "wt", 0, ["wt"], ["qw"])
-        pick(nt, 0, nw, 0, 128, "ln", 0, [nw + ".m"], [nw + ".m_s"], ["ln"], nt, nt + "_s")
+            act(T.pd[:, :], T.pob[:, :].indirect(T.dupl[:, :]), F.Copy, ["pob", "dupl"], ["pd"])
+        done = ((), (0, 1), (2,))[t]
+        for i in done:
+            m, nt = "mw%d" % (i + 1), "nt%d" % i
+            pick(nt, 0, m, 0, 128, "ln", 0, [m + ".m"], [m + ".m_s"], ["ln"], nt, nt + "_s")
         if last:
-            dmas([("y", T.oc[:, :], view(T, nt, 0, 128, True))], "st", [nt], ())
-            act(T.ups[:, :], T.zb3[:, 0:128], F.Copy, ["zb3"], ["ups"])
-            dmas([("y", T.osc[4 * k:4 * k + 4, :], T[nt + "_s"][32 * k:32 * k + 4, :]) for k in range(4)], "st", [nt + "_s"], ())
-            cp(T.upn[:, :], T.ups[:, :].indirect(T.ln[:, :]), ["ups", "ln"], ["upn"])
-            dmas([("y", T.up[:, :], T.upn[0:1, :])], "st", ["upn"], ())
-        for o in range(O):
-            mm("zb%d" % o, "qw", 128 * o, nt, 0, True, True, ["qw", nt, nt + "_s"])
-        act(T[ys][:, 0:128], T.zb0[:, 0:128], F.Copy, ["zb0"], [ys + ".0"])
-        cp(T[ys][:, 128:256], T.zb1[:, 0:128], ["zb1"], [ys + ".1"])
-        if t == 0:
-            fill(T.gb2[:, :], 0.0, (), ["gb2"])
+            dmas([("y", T.oc[:, :], view(T, "nt2", 0, 128, True))], "st", ["nt2"], ())
+            dmas([("y", T.osc[4 * k:4 * k + 4, :], T["nt2_s"][32 * k:32 * k + 4, :]) for k in range(4)], "st", ["nt2_s"], ())
+            quant("qg2", 0, 128, "gb2", 0, ["gb2d"], ["qg2"])
+        for i in done:
+            nt, z0, z1 = "nt%d" % i, "zb%d" % (2 * i % 4), "zb%d" % (2 * i % 4 + 1)
+            mm(z0, "qw", 0, nt, 0, True, True, ["qw", nt, nt + "_s"])
+            mm(z1, "qw", 128, nt, 0, True, True, ["qw", nt, nt + "_s"])
+            act(T["ys%d" % i][:, 0:128], T[z0][:, 0:128], F.Copy, [z0], ["ys%d.0" % i])
+            cp(T["ys%d" % i][:, 128:256], T[z1][:, 0:128], [z1], ["ys%d.1" % i])
         if not last:
             prefill_b()
-            dmas([("y", T.y[:, 256 * t:256 * t + 256], T[ys][:, :])], "st", [ys + ".0", ys + ".1"], ())
+            for i in done:
+                dmas([("y", T.y[:, 256 * i:256 * i + 256], T["ys%d" % i][:, :])], "st", ["ys%d.0" % i, "ys%d.1" % i], ())
             ni = "iw%d" % (t + 1)
             pick(ni, 0, iw, 0, 256, "rl%d" % t, 0, [iw + ".m", iw + ".c"], [iw + ".m_s", iw + ".c_s"], ["rl%d" % t], ni + ".m", ni + ".m_s")
         else:
-            dmas([("s", T.y[:, 256 * t:256 * t + 128], T[ys][:, 0:128])], "st", [ys + ".0"], ())
-            dmas([("y", T.y[:, 256 * t + 128:256 * t + 256], T[ys][:, 128:256])], "st", [ys + ".1"], ())
+            dmas([("s", T.y[:, 256 * t:256 * t + 128], T["ys%d" % t][:, 0:128])], "st", ["ys%d.0" % t], ())
+            dmas([("y", T.y[:, 256 * t + 128:256 * t + 256], T["ys%d" % t][:, 128:256])], "st", ["ys%d.1" % t], ())
+            mm("zb3", "pc", 0, "qg2", 0, True, True, ["pc", "qg2"])
+            act(T.ups[:, :], T.zb3[:, 0:128], F.Copy, ["zb3"], ["ups"])
+            dmas([("s", T.up[:, :], T.ups[0:1, :])], "st", ["ups"], ())
     for s, n in sorted(count.items()):
         g.wait_ge(T.sem[s], n)

@@ -4,6 +4,7 @@ from concourse.mybir import dt, AluOpType as A, AxisListType, ActivationFunction
 N, V, E, R, O, K = 8, 32, 128, 3, 2, 16
 X4, U8, U16, BF, F32, I32 = "float8_e4m3fn_x4", "uint8", "uint16", "bfloat16", "float32", "int32"
 EPS = 2.0 ** -120
+BIG = 1.5 * 2.0 ** 30
 SCRATCH = {}
 
 
@@ -15,31 +16,31 @@ for _i in range(4):
     _buf("zb%d" % _i, 512, F32, "psum")
     _buf("db%d" % _i, 512, F32, "psum")
 for _n, _c, _d in (
-        ("wr", 10, I32), ("mb", 672, BF), ("uc", 4, BF), ("wt", 1024, BF), ("pw", 512, BF),
-        ("one", 128, BF), ("idb", 128, BF), ("eb", 516, BF), ("nb", 516, BF), ("pb", 512, BF), ("gb", 512, BF), ("gb2", 512, BF), ("ub", 512, BF),
-        ("im16", 128, F32), ("pa", 128, F32), ("ij", 128, BF), ("ki", 8, I32), ("kf", 8, F32), ("cf", 112, F32), ("li", 40, I32), ("lff", 52, F32),
-        ("sm", 12, F32), ("tt", 48, F32),
-        ("sgl", 2, U16), ("dupl", 16, U16), ("ls", 8, U16), ("lb", 8, U16), ("fd", 48, U16), ("lf", 24, U16), ("ln", 8, U16),
-        ("ah", 128, BF), ("hd", 128, BF), ("mk", 128, BF), ("cu", 128, BF), ("jk", 128, BF), ("jb", 8, BF),
-        ("ar", 128, F32), ("rb", 128, F32), ("js", 512, BF), ("asl", 128, BF), ("slb", 128, BF),
-        ("ft", 24, F32), ("fk", 24, F32), ("dk", 768, BF), ("dkt", 768, BF),
-        ("pob", 128, BF), ("pd", 256, BF), ("pdt", 256, BF), ("ups", 128, F32), ("pn", 128, BF),
+        ("wr", 10, I32), ("mb", 768, BF), ("uc", 4, BF), ("wt", 1024, BF), ("pw", 512, BF),
+        ("one", 128, BF), ("ij", 128, BF), ("eb", 516, BF), ("nb", 516, BF), ("pb", 512, BF), ("gb", 512, BF), ("ub", 512, BF), ("pk", 512, BF), ("pn", 512, BF),
+        ("im16", 128, BF), ("pa", 128, F32), ("t1", 64, F32), ("c32", 32, F32), ("k24", 24, F32),
+        ("ki", 10, I32), ("ku", 10, U16), ("kf", 12, F32), ("cf", 112, F32), ("hx", 34, F32), ("lff", 24, F32), ("sm", 8, F32), ("tt", 48, F32),
+        ("li", 32, I32), ("ld", 32, I32), ("l4", 32, I32), ("fw", 72, F32), ("ls", 16, U16), ("fd", 24, U16), ("lf", 24, U16), ("ln", 16, U16),
+        ("ah", 128, BF), ("mk", 128, BF), ("cu", 128, BF), ("jk", 136, BF),
+        ("ar", 128, F32), ("rb", 128, F32), ("js", 512, BF), ("asl", 128, BF), ("slb", 128, BF), ("dk", 384, BF), ("dkt", 384, BF),
+        ("eq", 16, I32), ("ei", 2, I32), ("ef", 4, F32), ("oh", 16, F32), ("hk", 256, BF),
+        ("yv0", 128, F32), ("yv1", 128, F32), ("yw0", 256, F32), ("yw1", 256, F32), ("ups", 128, F32),
         ("z", 512, BF), ("dd", 512, BF), ("sx", 128, F32)):
     _buf(_n, _c, _d)
-for _n, _c in (("qmb", 160), ("qx", 128), ("qp", 128), ("bb", 128), ("ep", 512), ("en", 512), ("pc", 128), ("qg", 128), ("qg2", 128), ("qu", 128), ("qw", 256), ("qd", 128),
-               ("mw0", 256), ("mw1", 256), ("mw2", 256), ("mw3", 128), ("iw0", 256), ("iw1", 256), ("iw2", 128),
-               ("rm0", 32), ("rc0", 64), ("rc1", 64), ("f0", 384), ("f1", 384), ("f2", 384), ("nt0", 128), ("nt1", 128), ("nt2", 128)):
+for _n, _c in (("qmb", 160), ("qx", 128), ("qp", 128), ("bb", 128), ("ep", 512), ("en", 512), ("pc", 128), ("qg", 128), ("qk", 128), ("qn", 128), ("qu", 128), ("qw", 256), ("qd", 128),
+               ("mw0", 256), ("mw1", 256), ("mw2", 256), ("iw0", 256), ("iw1", 256), ("iw2", 128),
+               ("rm0", 32), ("rc0", 64), ("rc1", 64), ("f0", 384), ("f1", 384), ("f2", 384), ("nt", 128)):
     _buf(_n, _c, X4)
     _buf(_n + "_s", _c, U8)
 for _t in range(R):
-    _buf("lst%d" % _t, 16, U16)
     _buf("ys%d" % _t, 256, F32)
 for _t in range(R - 1):
+    _buf("lst%d" % _t, 16, U16)
     _buf("rl%d" % _t, 8, U16)
     _buf("rq%d" % _t, 2, U16)
 
 STAGES = ["m0", "m0s", "c0", "c0s", "l0", "c1", "c1s", "l1"]
-SEMAPHORES = ["qv", "qs", "qt", "qg", "ls", "lf", "ldr", "ldm", "ldu", "ldw", "hm0", "hc0", "hc1", "hl0", "hl1", "st"]
+SEMAPHORES = ["qv", "qs", "qt", "qg", "ls", "lf", "ldr", "ldm", "ldu", "ldw", "hm0", "hc0", "hc1", "hl0", "hl1", "st", "b_l0", "b_l1"]
 SEMAPHORES += ["a_" + s for s in STAGES] + ["r_" + s for s in STAGES]
 FAR, NEAR = 0, 1
 
@@ -69,6 +70,19 @@ def chips(T, topo, c):
         if not out or d not in topo.cores_of(out[-1][0]):
             out.append([])
         out[-1].append(d)
+    return out
+
+
+def runs(T, topo, c):
+    out = []
+    for r, d in enumerate(T.cores):
+        way = NEAR if d == c or topo.may_write(d, c) else FAR
+        if out and out[-1][2] == way:
+            out[-1][1] += 1
+        else:
+            out.append([r, 1, way])
+    if any(r % 2 for r, _, _ in out):
+        out = [[0, N, FAR]]
     return out
 
 
@@ -133,13 +147,21 @@ def onward(T, topo, x, stage):
     return out
 
 
+def arrival(stage, way):
+    return ("b_" if stage[0] == "l" and way == FAR else "a_") + stage
+
+
 def landed(T, topo, c, stage):
-    n = 0
+    n = {}
+    rank = T.rank_of(c) is not None
     for s in T.cores:
         if s != c:
-            n += sum(len(e) for way in (FAR, NEAR) for x, e, _ in roads(T, topo, s, stage, way) if x == c)
-        if T.rank_of(c) is not None and s == peers(T, topo, s)[0] and not topo.may_write(s, c):
-            n += sum(len(o[1]) for x in topo.cores_of(s) if T.rank_of(x) is None for o in onward(T, topo, x, stage) if o[0] == c)
+            for way in (FAR, NEAR):
+                k = arrival(stage, way) if rank else "r_" + stage
+                n[k] = n.get(k, 0) + sum(len(e) for x, e, _ in roads(T, topo, s, stage, way) if x == c)
+        if rank and s == peers(T, topo, s)[0] and not topo.may_write(s, c):
+            k = arrival(stage, FAR)
+            n[k] = n.get(k, 0) + sum(len(o[1]) for x in topo.cores_of(s) if T.rank_of(x) is None for o in onward(T, topo, x, stage) if o[0] == c)
     return n
 
 
@@ -163,9 +185,9 @@ def relay_program(g, core, T, topo):
             else:
                 src, dst = view(T, "r" + st[:2] + tail, K * a, K * n, codes), view(T, "iw%d" % t + tail, base + K * r, K * n, codes)
             rid, pid = topo.addr(d, core)
-            tr.append(RemoteDMATransfer(dst_ids=[DstId(rid=rid, pnc=pid)], dma_engine_mask=bits(e), remote_sem=T.sem["a_" + st], src=src, dst=dst))
+            tr.append(RemoteDMATransfer(dst_ids=[DstId(rid=rid, pnc=pid)], dma_engine_mask=bits(e), remote_sem=T.sem[arrival(st, FAR)], src=src, dst=dst))
             total += len(e)
-        g.wait_ge(T.sem["r_" + st], landed(T, topo, core, st))
+        g.wait_ge(T.sem["r_" + st], landed(T, topo, core, st)["r_" + st])
         g.remote_dma_fused(tr, local_sem=T.sem["ls"])
     if total:
         g.wait_ge(T.sem["ls"], total)
@@ -248,9 +270,9 @@ def rank_program(g, core, T, topo):
     def quant(name, a, b, tile, x, rd, wr):
         op("v", lambda: v.quantize_mx(T[name][:, a:b], T[name + "_s"][:, a:b], T[tile][:, x:x + 4 * (b - a)]), rd, wr)
 
-    def pick(out, a, src, c, d, off, e, codes, scales, lists, wc, ws):
-        op("v", lambda: v.tensor_copy(T[out][:, a:a + 128].bitcast(u32), T[src][:, c:d].bitcast(u32).indirect(T[off][:, e:e + 8])), codes + lists, [wc])
-        op("s", lambda: sc.activation(T[out + "_s"][:, a:a + 128], T[src + "_s"][:, c:d].indirect(T[off][:, e:e + 8]), F.Copy), scales + lists, [ws])
+    def pick(out, a, n, src, c, d, off, e, codes, scales, lists, wc, ws):
+        op("v", lambda: v.tensor_copy(T[out][:, a:a + n].bitcast(u32), T[src][:, c:d].bitcast(u32).indirect(T[off][:, e:e + n // K])), codes + lists, [wc])
+        op("s", lambda: sc.activation(T[out + "_s"][:, a:a + n], T[src + "_s"][:, c:d].indirect(T[off][:, e:e + n // K]), F.Copy), scales + lists, [ws])
 
     def mm(bank, ln, la, rn, ra, start, stop, rd):
         op("t", lambda: te.matmul_mx(T[bank][:, 0:128], T[ln][:, la:la + 128], T[ln + "_s"][:, la:la + 128],
@@ -265,57 +287,62 @@ def rank_program(g, core, T, topo):
     dmas([("y", T.uc[:, :], T.u[:, 0:4])], "ldu", (), ["uc"])
     dmas([("y", T.wt[:, :], T.w[:, :])], "ldw", (), ["wt"])
 
-    fill(T.one[:, :], 1.0, (), ["one"])
     op("g", lambda: g.iota(T.ki[:, 0:2], [[0, 2]], 0, 1), (), ["ip"])
     iota(T.im16[:, :], [[0, 8], [1, 16]], 0, "im16")
+    iota(T.t1[:, 32:64], [[128, 2], [0, 16]], 0, "tq")
+    iota(T.ij[:, :], [[1, 128]], 0, "ij")
+    iota(T.c32[:, :], [[1, 2], [1, 16]], 0, "c32")
+    iota(T.mb[:, 640:768], [[0, 128]], 0, "xz")
     iota(T.cf[:, 0:16], [[0, 2], [1, 8]], 0, "c8")
-    iota(T.mb[:, 640:672], [[0, 32]], 0, "xz")
-    iota(T.pb[:, :], [[0, 512]], 0, "pb", 1)
-    op("g", lambda: g.affine_select(T.eb[:, 0:512], T.pb[:, :], [[-1, 512]], A.is_equal, 0.0, 3, 4), ["pb"], ["eb0"])
-    iota(T.eb[:, 512:516], [[0, 4]], 0, "eb1")
-    tsc(T.ki[:, 2:4], T.ki[:, 0:2], 15, None, A.bitwise_and, None, ["ip"], ["kci"])
-    tsc(T.ki[:, 4:6], T.ki[:, 0:2], 4, None, A.logical_shift_right, None, ["ip"], ["gci"])
-    cp(T.kf[:, 0:2], T.ki[:, 2:4], ["kci"], ["kcf"])
-    fill(T.pw[:, :], 0.0, (), ["pw"])
-    tsc(T.kf[:, 4:6], T.ki[:, 2:4], 0.5, None, A.add, None, ["kci"], ["khf"])
-    cp(T.kf[:, 2:4], T.ki[:, 4:6], ["gci"], ["gcf"])
-    k16, g16, k05 = T.kf[:, 0:1], T.kf[:, 2:3], T.kf[:, 4:5]
-    act(T.pa[:, :], T.im16[:, :], F.Abs, ["im16", "kcf"], ["pa"], scale=-1.0, bias=k16)
-    for i, c in enumerate((0.5, 8.0)):
-        act(T.pw[:, i:512:4], T.pa[:, :], F.Relu, ["pa", "pw"], ["pw%d" % i], scale=-c, bias=c)
-    act(T.cf[:, 48:64], T.im16[:, 0:16], F.Relu, ["im16", "kcf"], ["below"], scale=-1.0, bias=k16)
-    act(T.cf[:, 96:112], T.cf[:, 0:16], F.Abs, ["c8", "gcf"], ["away"], scale=-1.0, bias=g16)
-    act(T.cf[:, 80:96], T.cf[:, 48:64], F.Sign, ["below"], ["lt"])
-    act(T.cf[:, 32:48], T.cf[:, 96:112], F.Relu, ["away"], ["hm"], scale=-8.0, bias=8.0)
-    act(T.cf[:, 64:80], T.cf[:, 80:96], F.Copy, ["lt"], ["mth"], scale=-2.0 ** -24, bias=1.0)
+    iota(T.k24[:, :], [[1, 3], [0, 8]], 0, "k24")
+    fill(T.eb[:, :], 0.0, (), ["ebz"])
+    fill(T.one[:, :], 1.0, (), ["one"])
+    tsc(T.ki[:, 2:4], T.ki[:, 0:2], 15, None, A.bitwise_and, None, ["ip"], ["i2"])
+    tsc(T.ki[:, 4:6], T.ki[:, 0:2], 4, None, A.logical_shift_right, None, ["ip"], ["i4"])
+    tsc(T.ki[:, 6:8], T.ki[:, 0:2], 22, None, A.bitwise_and, None, ["ip"], ["i6"])
+    tsc(T.ki[:, 8:10], T.ki[:, 0:2], 5, None, A.logical_shift_right, None, ["ip"], ["i8"])
+    cp(T.kf[:, 0:10], T.ki[:, :], ["ip", "i2", "i4", "i6", "i8"], ["kf"])
+    tsc(T.kf[:, 11:12], T.ki[:, 8:9], 256.0, BIG, A.mult, A.add, ["i8"], ["kc"])
+    tsc(T.t1[:, 0:32], T.t1[:, 32:64], T.kf[:, 11:12], None, A.add, None, ["tq", "kc"], ["t1"])
+    tsc(T.kf[:, 10:11], T.ki[:, 2:3], 0.5, None, A.add, None, ["i2"], ["kh"])
+    cp(T.ku[:, :], T.ki[:, :], ["ip", "i2", "i4", "i6", "i8"], ["ku"])
+    p1, k16, g16, k05 = T.kf[:, 0:1], T.kf[:, 2:3], T.kf[:, 4:5], T.kf[:, 10:11]
+    act(T.pa[:, :], T.im16[:, :], F.Abs, ["im16", "kf"], ["pa"], scale=-1.0, bias=k16)
+    for i, c in enumerate((0.5, 8.0, 0.5, 0.5)):
+        act(T.pw[:, i:512:4], T.pa[:, :], F.Relu, ["pa"], ["pw%d" % i], scale=-c, bias=c)
 
-    tsc(T.li[:, 0:4], T.wr[:, 1:9:2], 7, None, A.logical_shift_right, None, ["wr"], ["h4i"])
-    cp(T.lff[:, 0:4], T.li[:, 0:4], ["h4i"], ["h4f"])
-
-    def spread(dst, col, name, rd, both):
+    def spread(dst, col, rd, both):
         for b in range(4):
-            x = T.lff[:, col + b:col + b + 1]
+            o, x = T[dst][:, 32 * b:32 * b + 32], T.lff[:, col + b:col + b + 1]
             if both and b % 2:
-                act(T[dst][:, 32 * b:32 * b + 32], T.one[:, 0:32], F.Copy, ["one", rd], [dst + ".%d" % b], scale=x)
+                tsc(o, T.one[:, 0:32], x, None, A.mult, None, ["one", rd], [dst + ".%d" % b])
             else:
-                tsc(T[dst][:, 32 * b:32 * b + 32], T.one[:, 0:32], x, None, A.mult, None, ["one", rd], [dst + ".%d" % b])
-        turn(T[name][:, :], T[dst][:, :], [dst + ".%d" % b for b in range(4)], [name])
+                act(o, T.one[:, 0:32], F.Copy, ["one", rd], [dst + ".%d" % b], scale=x)
 
-    spread("ah", 0, "hd", "h4f", False)
-    tsc(T.mk[:, :], T.hd[:, :], g16, None, A.is_equal, None, ["hd", "gcf"], ["mk"])
+    tsc(T.lff[:, 0:4], T.wr[:, 1:9:2], 63.75, BIG, A.subtract, A.add, ["wr"], ["h4"])
+    for b in range(4):
+        tsc(T.ah[:, 32 * b:32 * b + 32], T.t1[:, 0:32], T.lff[:, b:b + 1], None, A.is_equal, None, ["t1", "h4"], ["ah%d" % b])
+    turn(T.mk[:, :], T.ah[:, :], ["ah%d" % b for b in range(4)], ["mk"])
     op("v", lambda: v.tensor_tensor_scan(T.cu[:, :], T.mk[:, :], T.mk[:, :], 0.0, A.add, A.max), ["mk"], ["cu"])
-    act(T.jb[:, :], T.cu[:, 15:128:16], F.Sign, ["cu", "khf"], ["jb", "acc1"], scale=-1.0, bias=k05, accum_out=T.lff[:, 17:18])
-    act(T.jk[:, :], T.cu[:, :], F.Sign, ["cu", "khf"], ["jk", "acc0"], scale=-1.0, bias=k05, accum_out=T.lff[:, 16:17])
-    quant("qp", 0, 128, "pw", 0, ["pw", "pw0", "pw1"], ["qp"])
-    quant("qmb", 0, 160, "mb", 0, ["mb"], ["qmb"])
-    tsc(T.mb[:, 641:672:4], T.cf[:, 0:8], g16, T.lff[:, 17:18], A.is_equal, A.mult, ["c8", "gcf", "acc1", "xz"], ["x1"])
-    tsc(T.lff[:, 18:19], T.lff[:, 17:18], -16.0, T.lff[:, 16:17], A.mult, A.add, ["acc0", "acc1"], ["low"])
-    tsc(T.mb[:, 640:672:4], T.cf[:, 0:8], g16, T.lff[:, 18:19], A.is_equal, A.mult, ["c8", "gcf", "low", "xz"], ["x0"])
-    quant("qx", 0, 128, "mb", 160, ["mb", "xz", "x0", "x1"], ["qx"])
-    mm("db0", "qp", 0, "qx", 0, True, True, ["qp", "qx"])
-    tsc(T.ls[:, :], T.db0[:, 120:128], 64.0, None, A.add, None, ["db0"], ["ls"])
-    pick("mw0", 0, "qmb", 0, 128, "ls", 0, ["qmb"], ["qmb"], ["ls"], "mw0.m", "mw0.m_s")
+    act(T.jk[:, 128:136], T.cu[:, 15:128:16], F.Sign, ["cu", "kh"], ["jb", "acc1"], scale=-1.0, bias=k05, accum_out=T.lff[:, 17:18])
+    act(T.jk[:, 0:128], T.cu[:, :], F.Sign, ["cu", "kh"], ["jk", "acc0"], scale=-1.0, bias=k05, accum_out=T.lff[:, 16:17])
     cp(T.lff[:, 4:8], T.wr[:, 1:9:2], ["wr"], ["r4f"])
+    quant("qp", 0, 128, "pw", 0, ["pw%d" % i for i in range(4)], ["qp"])
+    tsc(T.mb[:, 641:768:4], T.c32[:, :], g16, T.lff[:, 17:18], A.is_equal, A.mult, ["c32", "kf", "acc1", "xz"], ["x1"])
+    tsc(T.lff[:, 18:19], T.lff[:, 17:18], -16.0, T.lff[:, 16:17], A.mult, A.add, ["acc0", "acc1"], ["low"])
+    tsc(T.mb[:, 640:768:4], T.c32[:, :], g16, T.lff[:, 18:19], A.is_equal, A.mult, ["c32", "kf", "low", "xz"], ["x0"])
+    quant("qx", 0, 128, "mb", 256, ["mb", "xz", "x0", "x1"], ["qx"])
+    mm("db0", "qp", 0, "qx", 0, True, True, ["qp", "qx"])
+    quant("qmb", 0, 160, "mb", 0, ["mb"], ["qmb"])
+    spread("ar", 4, "r4f", False)
+    act(T.cf[:, 48:64], T.im16[:, 0:16], F.Relu, ["im16", "kf"], ["below"], scale=-1.0, bias=k16)
+    act(T.cf[:, 96:112], T.cf[:, 0:16], F.Abs, ["c8", "kf"], ["away"], scale=-1.0, bias=g16)
+    act(T.cf[:, 80:96], T.cf[:, 48:64], F.Sign, ["below"], ["lt"])
+    act(T.hx[:, 0:16], T.cf[:, 96:112], F.Relu, ["away"], ["hm"], scale=-8.0, bias=8.0)
+    act(T.cf[:, 64:80], T.cf[:, 80:96], F.Copy, ["lt"], ["mth"], scale=-2.0 ** -24, bias=1.0)
+    act(T.lff[:, 20:24], T.uc[:, :], F.Copy, ["uc"], ["ucf"])
+    tsc(T.ls[:, 0:8], T.db0[:, 96:104], 64.0, None, A.add, None, ["db0"], ["ls"])
+    pick("mw0", 0, 128, "qmb", 0, 128, "ls", 0, ["qmb"], ["qmb"], ["ls"], "mw0.m", "mw0.m_s")
 
     def send(stage, way, src, rd, local="ls"):
         t, tail, codes, base = kind(stage)
@@ -332,10 +359,10 @@ def rank_program(g, core, T, topo):
                 dst = view(T, "r" + stage[:2] + tail, K * n * i, K * n, codes)
             rid, pid = topo.addr(x, core)
             tr.append(RemoteDMATransfer(dst_ids=[DstId(rid=rid, pnc=pid)], dma_engine_mask=bits(e),
-                                        remote_sem=T.sem[("a_" if way == NEAR else "r_") + stage], src=src(T.rank_of(ds[0]), n), dst=dst))
+                                        remote_sem=T.sem[arrival(stage, NEAR) if way == NEAR else "r_" + stage], src=src(T.rank_of(ds[0]), n), dst=dst))
             count[local] = count.get(local, 0) + len(e)
         g.remote_dma_fused(tr, local_sem=T.sem[local])
-        count["a_" + stage] = landed(T, topo, core, stage)
+        count.update(landed(T, topo, core, stage))
 
     def columns(stage, way, local="ls"):
         t, tail, codes, base = kind(stage)
@@ -356,50 +383,48 @@ def rank_program(g, core, T, topo):
             columns(st, way, local)
     wrote["left"] = [("lf", count["lf"])]
     home("m0", ["left"])
-    op("g", lambda: g.affine_select(T.idb[:, :], T.one[:, :], [[-1, 128]], A.is_equal, 0.0, 0, 1), ["one"], ["idb"])
-    iota(T.cf[:, 16:32], [[16, 8], [0, 2]], 0, "h16")
+    iota(T.pb[:, :], [[0, 512]], 0, "pb", 1)
+    iota(T.nb[:, :], [[0, 516]], 0, "nbz")
     iota(T.gb[:, :], [[0, 512]], 0, "gb")
-    iota(T.ij[:, :], [[1, 128]], 0, "ij")
-    iota(T.gb2[:, :], [[0, 512]], 0, "gb2")
+    iota(T.cf[:, 16:32], [[16, 8], [0, 2]], 0, "h16")
 
-    spread("ar", 4, "rb", "r4f", True)
+    turn(T.rb[:, :], T.ar[:, :], ["ar.%d" % b for b in range(4)], ["rb"])
     for b in range(4):
         act(T.js[:, 128 * b:128 * b + 128], T.rb[:, :], F.Sign, ["rb", "r4f"], ["js%d" % b, "sa%d" % b], scale=-1.0, bias=T.lff[:, 4 + b:5 + b], accum_out=T.lff[:, 8 + b:9 + b])
-    act(T.pb[:, 0:512:4], T.pa[:, :], F.Relu, ["pa", "pb", "eb0"], ["pb0"], scale=-128.0, bias=128.0)
-    act(T.pb[:, 2:512:4], T.im16[:, :], F.Copy, ["im16", "pb", "eb0"], ["pb2"])
-    cp(T.li[:, 8:16], T.ls[:, :], ["ls"], ["lsi"])
-    tsc(T.li[:, 16:24], T.li[:, 8:16], 3, None, A.bitwise_and, None, ["lsi"], ["lqi"])
-    tsc(T.li[:, 24:32], T.li[:, 8:16], 124, None, A.bitwise_and, None, ["lsi"], ["l4i"])
-    tsc(T.li[:, 32:40], T.li[:, 8:16], 2, None, A.logical_shift_right, None, ["lsi"], ["lbi"])
-    for k in range(3):
-        tsc(T.ft[:, 8 * k:8 * k + 8], T.li[:, 16:24], float(k), float(k), A.is_le, A.add, ["lqi"], ["ft%d" % k])
-    for k in range(3):
-        ttn(T.fk[:, 8 * k:8 * k + 8], T.ft[:, 8 * k:8 * k + 8], T.li[:, 24:32], A.add, ["ft%d" % k, "l4i"], ["fk%d" % k])
-    cp(T.lb[:, :], T.li[:, 32:40], ["lbi"], ["lb"])
-    cp(T.fd[:, 0:48:2], T.fk[:, :], ["fk0", "fk1", "fk2"], ["fd0"])
-    cp(T.fd[:, 1:48:2], T.fk[:, :], ["fk0", "fk1", "fk2"], ["fd1"])
+    tsc(T.li[:, :], T.db0[:, 96:128], 64.0, None, A.add, None, ["db0"], ["li"])
+    cp(T.ld[:, :], T.li[:, :].indirect(T.ku[:, 6:8]), ["li", "ku"], ["ld"])
+    tsc(T.l4[:, 24:32], T.li[:, 0:8], 2, None, A.logical_shift_right, None, ["li"], ["l2"])
+    tsc(T.l4[:, 0:24], T.ld[:, 0:24], 124, None, A.bitwise_and, None, ["ld"], ["l4"])
+    cp(T.ls[:, 8:16], T.l4[:, 24:32], ["l2"], ["lb"])
+    ttn(T.fw[:, 0:24], T.l4[:, 0:24], T.k24[:, :], A.add, ["l4", "k24"], ["fw"])
+    ttn(T.fw[:, 24:48], T.fw[:, 0:24], T.ld[:, 0:24], A.is_ge, ["fw", "ld"], ["fc"])
+    ttn(T.fw[:, 48:72], T.fw[:, 0:24], T.fw[:, 24:48], A.add, ["fw", "fc"], ["fk"])
+    cp(T.fd[:, :], T.fw[:, 48:72], ["fk"], ["fd"])
+    pick("bb", 0, 128, "qmb", 128, 160, "ls", 8, ["qmb"], ["qmb"], ["lb"], "bb", "bb_s")
     tsc(T.lff[:, 12:16], T.lff[:, 8:12], 0.5, 63.5, A.mult, A.add, ["sa%d" % b for b in range(4)], ["s4"])
-    spread("asl", 12, "slb", "s4", True)
-    for k in range(3):
-        o, i = T.dk[:, 256 * k:256 * k + 256], T.slb[:, :].indirect(T.fd[:, 16 * k:16 * k + 16])
-        if k:
-            act(o, i, F.Copy, ["slb", "fd0", "fd1"], ["dk%d" % k])
-        else:
-            cp(o, i, ["slb", "fd0", "fd1"], ["dk%d" % k])
-    for k in range(3):
-        d0, d1 = 256 * k, 256 * k + 256
-        turn(T.dkt[:, d0:d1], T.dk[:, d0:d1], ["dk%d" % k], ["dkt%d" % k])
-        cp(T.lf[:, 8 * k:8 * k + 8], T.dkt[:, d0:d1:32], ["dkt%d" % k], ["lf%d" % k])
-    pick("bb", 0, "qmb", 128, 160, "lb", 0, ["qmb"], ["qmb"], ["lb"], "bb", "bb_s")
-    for b in range(4):
-        quant("ep", 128 * b, 128 * b + 128, "eb", 3 - b, ["eb0", "eb1"], ["ep%d" % b])
-    act(T.nb[:, :], T.eb[:, :], F.Copy, ["eb0", "eb1"], ["nb"], scale=-1.0)
-    act(T.lff[:, 48:52], T.uc[:, :], F.Copy, ["uc"], ["ucf"])
+    spread("asl", 12, "s4", True)
+    tsc(T.eb[:, 3:512:4], T.ij[:, :], p1, None, A.is_equal, None, ["ij", "kf", "ebz"], ["ebh"])
+    turn(T.slb[:, :], T.asl[:, :], ["asl.%d" % b for b in range(4)], ["slb"])
+    cp(T.dk[:, 0:192], T.slb[:, :].indirect(T.fd[:, 0:12]), ["slb", "fd"], ["dk0"])
+    act(T.dk[:, 192:384], T.slb[:, :].indirect(T.fd[:, 12:24]), F.Copy, ["slb", "fd"], ["dk1"])
+
+    def unpacking(b):
+        quant("ep", 128 * b, 128 * b + 128, "eb", 3 - b, ["ebz", "ebh"], ["ep%d" % b])
+
+    for b in (0, 1):
+        unpacking(b)
+    turn(T.dkt[:, :], T.dk[:, :], ["dk0", "dk1"], ["dkt"])
+    cp(T.lf[:, :], T.dkt[:, 0:384:16], ["dkt"], ["lf"])
+    for b in (2, 3):
+        unpacking(b)
+    act(T.pb[:, 0:512:4], T.pa[:, :], F.Relu, ["pa", "pb"], ["pb0"], scale=-128.0, bias=128.0)
+    act(T.pb[:, 2:512:4], T.im16[:, :], F.Copy, ["im16", "pb"], ["pb2"])
 
     def tile_u(t):
-        act(T.ub[:, t:512:4], T.one[:, :], F.Copy, ["one", "ucf"], ["ub%d" % t], scale=T.lff[:, 48 + t:49 + t])
+        act(T.ub[:, t:512:4], T.one[:, :], F.Copy, ["one", "ucf"], ["ub%d" % t], scale=T.lff[:, 20 + t:21 + t])
 
-    tile_u(0)
+    for b in (0, 1):
+        tile_u(b)
 
     def prefill_m(t):
         for b in range(4):
@@ -410,27 +435,39 @@ def rank_program(g, core, T, topo):
             mm("zb%d" % b, "ep", 128 * b, "bb", 0, True, False, ["ep%d" % b, "bb", "bb_s"])
 
     prefill_b()
+    seg = runs(T, topo, core)
+    flags = ["gb", "gb0", "gb1", "gb3", "gb4", "gb5", "gb6", "gb7"]
+
+    def inw(t, tail):
+        return ["iw%d.m%s" % (t, tail)] if t == 0 else ["iw%d.m%s.%d" % (t, tail, r) for r, _, _ in seg]
+
+    def results(i, src, m):
+        act(T["ys%d" % i][:, 0:128], T[src + "0"][:, 0:128].indirect(T.ln[:, 0:8]), F.Copy, [src + "0" + m, "ln"], ["ys%d.0" % i])
+        cp(T["ys%d" % i][:, 128:256], T[src + "1"][:, 0:128].indirect(T.ln[:, 0:8]), [src + "1" + m, "ln"], ["ys%d.1" % i])
+        dmas([("y", T.y[:, 256 * i:256 * i + 256], T["ys%d" % i][:, :])], "st", ["ys%d.0" % i, "ys%d.1" % i], ())
 
     for t in range(R):
-        iw, mw, f, lst = "iw%d" % t, "mw%d" % t, "f%d" % t, "lst%d" % t
+        iw, mw, f = "iw%d" % t, "mw%d" % t, "f%d" % t
         nw, last = "mw%d" % (t + 1), t == R - 1
         for k in range(3):
-            pick(f, 128 * k, iw, 0, 128, "lf", 8 * k, [iw + ".m"], [iw + ".m_s"], ["lf%d" % k], f + ".%d" % k, f + "s.%d" % k)
+            pick(f, 128 * k, 128, iw, 0, 128, "lf", 8 * k, inw(t, ""), inw(t, "_s"), ["lf"], f + ".%d" % k, f + "s.%d" % k)
         for k in range(3):
             for b in range(4):
                 mm("zb%d" % b, "ep", 128 * b, f, 128 * k, False, k == 2, ["ep%d" % b, f + ".%d" % k, f + "s.%d" % k])
         if t == 0:
+            tsc(T.nb[:, 3:512:4], T.ij[:, :], p1, -1.0, A.is_equal, A.mult, ["ij", "kf", "nbz"], ["nbh"])
             for b in range(4):
-                quant("en", 128 * b, 128 * b + 128, "nb", 3 - b, ["nb"], ["en%d" % b])
+                quant("en", 128 * b, 128 * b + 128, "nb", 3 - b, ["nbz", "nbh"], ["en%d" % b])
             prefill_m(0)
-            cp(T.sgl[:, :], T.ki[:, 0:2], ["ip"], ["sgl"])
-            for b in range(1, 4):
+            for b in (2, 3):
                 tile_u(b)
+            act(T.ub[:, 4:8], T.uc[:, :], F.Copy, ["uc"] + ["ub%d" % b for b in range(4)], ["ubn"], scale=-1.0)
         if t == 1:
-            turn(T.pdt[:, :], T.pd[:, :], ["pd"], ["pdt"])
+            quant("qk", 0, 128, "pk", 0, ["pk%d" % i for i in range(4)], ["qk"])
             quant("qw", 0, 256, "wt", 0, ["wt"], ["qw"])
-            cp(T.ln[:, :], T.pdt[:, 0:256:32], ["pdt"], ["ln"])
-            act(T.pn[:, :], T.idb[:, :].indirect(T.ln[:, :]), F.Copy, ["idb", "ln"], ["pn"])
+        if last:
+            quant("qn", 0, 128, "pn", 0, ["pnz", "pn0", "pn3"], ["qn"])
+            results(1, "yw", ".m")
         for b in range(4):
             if b % 2:
                 tsc(T.z[:, b:512:4], T["zb%d" % b][:, 0:128], 0.25, None, A.mult, None, ["zb%d" % b], ["z%d" % b])
@@ -440,7 +477,7 @@ def rank_program(g, core, T, topo):
         for b in range(4):
             mm("db%d" % b, "ep", 128 * b, mw, 128, False, True, ["ep%d" % b, mw + ".c"])
         if t == 0:
-            quant("qu", 0, 128, "ub", 0, ["ub%d" % b for b in range(4)], ["qu"])
+            quant("qu", 0, 128, "ub", 0, ["ubn"] + ["ub%d" % b for b in range(4)], ["qu"])
             quant("pc", 0, 128, "pb", 0, ["pb", "pb0", "pb2"], ["pc"])
             act(T.gb[0:1, 1:32:4], T.one[0:1, 0:8], F.Copy, ["one", "gb"], ["gb1"], scale=float(K * rank))
             act(T.gb[0:1, 33:64:4], T.cf[0:1, 16:32:2], F.Copy, ["h16", "gb"], ["gb3"])
@@ -455,61 +492,92 @@ def rank_program(g, core, T, topo):
             else:
                 act(T.dd[:, b:512:4], T["db%d" % b][:, 0:128], F.Copy, ["db%d" % b], ["dd%d" % b])
         quant("qd", 0, 128, "dd", 0, ["dd%d" % b for b in range(4)], ["qd"])
-        mm("zb0", "qd", 0, "qu", 0, True, True, ["qu", "qd"])
+        if last:
+            for o in range(O):
+                mm("zb%d" % (2 + o), "qw", 128 * o, mw, 128, True, True, ["qw", mw + ".c"])
+            cp(T.yw0[:, 128:256], T.zb2[:, 0:128], ["zb2"], ["yw0.c"])
         mm("zb1", "qu", 0, "qd", 0, True, True, ["qu", "qd"])
-        act(T.sm[:, 0:1], T.zb0[:, 0:1], F.Abs, ["zb0"], ["sc"], bias=EPS)
+        mm("zb0", "qd", 0, "qu", 0, True, True, ["qu", "qd"])
         act(T.sx[:, :], T.zb1[:, 0:128], F.Abs, ["zb1"], ["sx"], bias=EPS)
+        tsc(T.sm[:, 0:1], T.zb0[:, 0:1], T.zb0[:, 1:2], EPS, A.max, A.add, ["zb0"], ["sc"])
         tsc(T.tt[:, 16:32], T.cf[:, 64:80], T.sm[:, 0:1], None, A.mult, None, ["mth", "sc"], ["th"])
-        ttn(T.tt[:, 32:48], T.sx[:, :].indirect(T.sgl[:, 0:1]), T.tt[:, 16:32], A.is_gt, ["sx", "sgl", "th"], ["kk"])
+        ttn(T.tt[:, 32:48], T.sx[:, :].indirect(T.ku[:, 0:1]), T.tt[:, 16:32], A.is_gt, ["sx", "ku", "th"], ["kk"])
         op("v", lambda: v.tensor_reduce(T.sm[:, 2:3], T.tt[:, 32:48], AxisListType.X, A.add), ["kk"], ["rk"])
-        tsc(T.gb[:, 0:64:4], T.cf[:, 32:48], T.sm[:, 2:3], None, A.is_gt, None, ["hm", "rk", "gb"], ["gb0"])
-        quant("qg", 0, 128, "gb", 0, ["gb0", "gb1", "gb3", "gb4"], ["qg"])
+        if t == 0:
+            tsc(T.gb[:, 0:64:4], T.hx[:, 0:16], T.sm[:, 2:3], None, A.is_gt, None, ["hm", "rk", "gb"], ["gb0"])
+        else:
+            tsc(T.gb[:, 0:132:4], T.hx[:, 0:33], T.sm[:, 2:3], None, A.is_gt, None, ["hm", "hn", "h0", "h8", "rk", "gb"], ["gb0"])
+        quant("qg", 0, 128, "gb", 0, flags, ["qg"])
+        if last:
+            act(T.yw1[:, 128:256], T.zb3[:, 0:128], F.Copy, ["zb3"], ["yw1.c"])
+            mm("db0", "qk", 0, "qg", 0, True, True, ["qk", "qg"])
+            mm("db1", "qg", 0, "qn", 0, True, True, ["qg", "qn"])
+            cp(T.ln[:, 8:16], T.db0[:, 16:24], ["db0"], ["nl"])
+            pick("nt", 0, 128, mw, 0, 256, "ln", 8, [mw + ".m", mw + ".c"], [mw + ".m_s", mw + ".c_s"], ["nl"], "nt", "nt_s")
+            act(T.ys2[:, 0:128], T.yw0[:, :].indirect(T.ln[:, 8:16]), F.Copy, ["yw0.m", "yw0.c", "nl"], ["ys2.0"])
+            cp(T.ys2[:, 128:256], T.yw1[:, :].indirect(T.ln[:, 8:16]), ["yw1.m", "yw1.c", "nl"], ["ys2.1"])
+            cp(T.ups[:, :], T.db1[:, 0:128], ["db1"], ["ups"])
+            dmas([("y", T.oc[:, :], view(T, "nt", 0, 128, True))], "st", ["nt"], ())
+            dmas([("y", T.osc[4 * k:4 * k + 4, :], T["nt_s"][32 * k:32 * k + 4, :]) for k in range(4)], "st", ["nt_s"], ())
+            dmas([("s", T.y[:, 512:640], T.ys2[:, 0:128])], "st", ["ys2.0"], ())
+            dmas([("y", T.y[:, 640:768], T.ys2[:, 128:256])], "st", ["ys2.1"], ())
+            dmas([("s", T.up[:, :], T.ups[32:33, :])], "st", ["ups"], ())
+            break
+        lst = "lst%d" % t
         mm("zb2", "pc", 0, "qg", 0, True, True, ["pc", "qg"])
         if t == 0:
-            tsc(T.sm[:, 5:6], T.sm[:, 2:3], 8.0, None, A.is_lt, None, ["rk"], ["cnt1"])
-        else:
-            tsc(T.sm[:, 5 + t:6 + t], T.sm[:, 2:3], 8.0, T.sm[:, 4 + t:5 + t], A.is_lt, A.add, ["rk", "cnt%d" % t], ["cnt%d" % (t + 1)])
+            tsc(T.sm[:, 6:7], T.sm[:, 2:3], 8.0, None, A.is_lt, None, ["rk"], ["cnt"])
         cp(T[lst][:, :], T.zb2[:, 0:16], ["zb2"], [lst])
-        if not last:
-            for way in (FAR, NEAR):
-                send("l%d" % t, way, lambda h, n: T[lst][:, h:h + n], [lst])
-            dmas([("y", T["rl%d" % t][:, rank:rank + 1], T[lst][:, rank:rank + 1])], "hl%d" % t, [lst], ["home"])
-            wrote["rl%d" % t] = [("a_l%d" % t, count["a_l%d" % t])] + wrote.pop("home")
-            home("c%d" % t, [lst])
-        else:
-            act(T.gb2[:, 3:512:4], T.pn[:, :], F.Copy, ["pn", "gb2", "cnt%d" % R], ["gb2d"], scale=T.sm[:, 4 + R:5 + R])
-        pick(nw, 0, mw, 0, 256, lst, 8, [mw + ".m", mw + ".c"], [mw + ".m_s", mw + ".c_s"], [lst], nw + ".m", nw + ".m_s")
-        if not last:
-            prefill_m(t + 1)
+        for way in (FAR, NEAR):
+            send("l%d" % t, way, lambda h, n: T[lst][:, h:h + n], [lst])
+        dmas([("y", T["rl%d" % t][:, rank:rank + 1], T[lst][:, rank:rank + 1])], "hl%d" % t, [lst], ["home"])
+        h = wrote.pop("home")
+        for way in (FAR, NEAR):
+            s = arrival("l%d" % t, way)
+            wrote["rl%d.%d" % (t, way)] = [(s, count[s])] + (h if way == NEAR else [])
+        if len(seg) == 1:
+            wrote["rl%d.%d" % (t, FAR)] += wrote["rl%d.%d" % (t, NEAR)]
+        home("c%d" % t, [lst])
+        pick(nw, 0, 128, mw, 0, 256, lst, 8, [mw + ".m", mw + ".c"], [mw + ".m_s", mw + ".c_s"], [lst], nw + ".m", nw + ".m_s")
+        prefill_m(t + 1)
         if t == 0:
-            cp(T.pob[:, :].indirect(T.ls[:, :]), T.ij[:, :], ["ls", "ij"], ["pob"])
-            tsc(T.dupl[:, :], T.cf[:, 16:32], k16, None, A.add, None, ["h16", "kcf"], ["dupl"])
-            act(T.pd[:, :], T.pob[:, :].indirect(T.dupl[:, :]), F.Copy, ["pob", "dupl"], ["pd"])
-        done = ((), (0, 1), (2,))[t]
-        for i in done:
-            m, nt = "mw%d" % (i + 1), "nt%d" % i
-            pick(nt, 0, m, 0, 128, "ln", 0, [m + ".m"], [m + ".m_s"], ["ln"], nt, nt + "_s")
-        if last:
-            dmas([("y", T.oc[:, :], view(T, "nt2", 0, 128, True))], "st", ["nt2"], ())
-            dmas([("y", T.osc[4 * k:4 * k + 4, :], T["nt2_s"][32 * k:32 * k + 4, :]) for k in range(4)], "st", ["nt2_s"], ())
-            quant("qg2", 0, 128, "gb2", 0, ["gb2d"], ["qg2"])
-        for i in done:
-            nt, z0, z1 = "nt%d" % i, "zb%d" % (2 * i % 4), "zb%d" % (2 * i % 4 + 1)
-            mm(z0, "qw", 0, nt, 0, True, True, ["qw", nt, nt + "_s"])
-            mm(z1, "qw", 128, nt, 0, True, True, ["qw", nt, nt + "_s"])
-            act(T["ys%d" % i][:, 0:128], T[z0][:, 0:128], F.Copy, [z0], ["ys%d.0" % i])
-            cp(T["ys%d" % i][:, 128:256], T[z1][:, 0:128], [z1], ["ys%d.1" % i])
-        if not last:
-            prefill_b()
-            for i in done:
-                dmas([("y", T.y[:, 256 * i:256 * i + 256], T["ys%d" % i][:, :])], "st", ["ys%d.0" % i, "ys%d.1" % i], ())
-            ni = "iw%d" % (t + 1)
-            pick(ni, 0, iw, 0, 256, "rl%d" % t, 0, [iw + ".m", iw + ".c"], [iw + ".m_s", iw + ".c_s"], ["rl%d" % t], ni + ".m", ni + ".m_s")
+            iota(T.pn[:, :], [[0, 512]], 0, "pnz")
+            iota(T.hx[:, 24:32], [[0, 8]], 0, "h0")
+            iota(T.hx[:, 32:34], [[0, 2]], 0, "h8", 8)
+            cp(T.eq[:, :], T.li[:, :].indirect(T.ku[:, 4:5]), ["li", "ku"], ["eq"])
+            tsc(T.ei[:, 0:1], T.eq[:, 0:1], 15, None, A.bitwise_and, None, ["eq"], ["e0"])
+            tsc(T.ei[:, 1:2], T.eq[:, 0:1], 4, None, A.logical_shift_right, None, ["eq"], ["e1"])
+            cp(T.ef[:, 0:2], T.ei[:, :], ["e0", "e1"], ["ef"])
+            tsc(T.hk[:, 0:128], T.im16[:, :], T.ef[:, 0:1], None, A.is_equal, None, ["im16", "ef"], ["hk"])
+            for i, c in enumerate((128.0, 16.0, 1.0, 1.0)):
+                act(T.pk[:, i:512:4], T.hk[:, 0:128], F.Copy, ["hk"], ["pk%d" % i], scale=c)
+            cp(T.ef[:, 2:3], T.eq[:, 0:1], ["eq"], ["ee"])
+            tsc(T.hk[:, 128:256], T.ij[:, :], T.ef[:, 2:3], None, A.is_equal, None, ["ij", "ee"], ["hnn"])
+            for i in (0, 3):
+                act(T.pn[:, i:512:4], T.hk[:, 128:256], F.Copy, ["hnn", "pnz"], ["pn%d" % i])
+            tsc(T.oh[:, :], T.cf[:, 0:16], T.ef[:, 1:2], None, A.is_equal, None, ["c8", "ef"], ["oh"])
+            tsc(T.hx[:, 16:24], T.oh[:, 0:8], 8.0, None, A.mult, None, ["oh"], ["hn"])
+            tsc(T.gb[:, 65:128:4], T.oh[:, :], g16, None, A.mult, None, ["oh", "kf", "gb", "qg"], ["gb6"])
+            tsc(T.gb[:, 66:128:4], T.oh[:, :], k16, None, A.mult, None, ["oh", "kf", "gb", "qg"], ["gb7"])
         else:
-            dmas([("s", T.y[:, 256 * t:256 * t + 128], T["ys%d" % t][:, 0:128])], "st", ["ys%d.0" % t], ())
-            dmas([("y", T.y[:, 256 * t + 128:256 * t + 256], T["ys%d" % t][:, 128:256])], "st", ["ys%d.1" % t], ())
-            mm("zb3", "pc", 0, "qg2", 0, True, True, ["pc", "qg2"])
-            act(T.ups[:, :], T.zb3[:, 0:128], F.Copy, ["zb3"], ["ups"])
-            dmas([("s", T.up[:, :], T.ups[0:1, :])], "st", ["ups"], ())
+            mm("zb3", "qk", 0, "qg", 0, True, True, ["qk", "qg"])
+            for o in range(O):
+                mm("zb%d" % o, "qw", 128 * o, mw, 0, True, True, ["qw", mw + ".m", mw + ".m_s"])
+            cp(T.ln[:, 0:8], T.zb3[:, 24:32], ["zb3"], ["ln"])
+            for o in range(O):
+                mm("zb%d" % (2 + o), "qw", 128 * o, nw, 0, True, True, ["qw", nw + ".m", nw + ".m_s"])
+            act(T.yv0[:, :], T.zb0[:, 0:128], F.Copy, ["zb0"], ["yv0"])
+            cp(T.yv1[:, :], T.zb1[:, 0:128], ["zb1"], ["yv1"])
+            act(T.yw0[:, 0:128], T.zb2[:, 0:128], F.Copy, ["zb2"], ["yw0.m"])
+            cp(T.yw1[:, 0:128], T.zb3[:, 0:128], ["zb3"], ["yw1.m"])
+            results(0, "yv", "")
+            tsc(T.gb[:, 131:132], T.sm[:, 2:3], 8.0, T.sm[:, 6:7], A.is_lt, A.add, ["rk", "cnt", "gb"], ["gb5"])
+        prefill_b()
+        ni = "iw%d" % (t + 1)
+        for way in (NEAR, FAR):
+            for r, n, w in seg:
+                if w == way:
+                    pick(ni, K * r, K * n, iw, 0, 256, "rl%d" % t, r, inw(t, "") + [iw + ".c"], inw(t, "_s") + [iw + ".c_s"],
+                         ["rl%d.%d" % (t, way)], ni + ".m.%d" % r, ni + ".m_s.%d" % r)
     for s, n in sorted(count.items()):
         g.wait_ge(T.sem[s], n)

from concourse.bass import DstId, RemoteDMATransfer
from concourse.mybir import dt, AluOpType as A, AxisListType, ActivationFunctionType as F

N, V, E, R, O, K = 8, 32, 128, 3, 2, 16
X4, U8, U16, BF, F32, I32 = "float8_e4m3fn_x4", "uint8", "uint16", "bfloat16", "float32", "int32"
EPS = 2.0 ** -120
BIG = 1.5 * 2.0 ** 30
SCRATCH = {}


def _buf(name, cols, dtype, where="sbuf"):
    SCRATCH[name] = (where, [128, cols], dtype)


for _i in range(4):
    _buf("zb%d" % _i, 512, F32, "psum")
    _buf("db%d" % _i, 512, F32, "psum")
for _n, _c, _d in (
        ("wr", 10, I32), ("mb", 768, BF), ("uc", 4, BF), ("wt", 1024, BF), ("pw", 512, BF),
        ("one", 128, BF), ("ij", 128, BF), ("eb", 516, BF), ("nb", 516, BF), ("pb", 512, BF), ("gb", 512, BF), ("ub", 512, BF), ("pk", 512, BF), ("pn", 512, BF),
        ("im16", 128, BF), ("pa", 128, F32), ("t1", 64, F32), ("c32", 32, F32), ("k24", 24, F32),
        ("ki", 10, I32), ("ku", 10, U16), ("kf", 12, F32), ("cf", 112, F32), ("hx", 34, F32), ("lff", 24, F32), ("sm", 8, F32), ("tt", 48, F32),
        ("li", 32, I32), ("ld", 32, I32), ("l4", 32, I32), ("fw", 72, F32), ("ls", 16, U16), ("fd", 24, U16), ("lf", 24, U16), ("ln", 16, U16),
        ("ah", 128, BF), ("mk", 128, BF), ("cu", 128, BF), ("jk", 136, BF),
        ("ar", 128, F32), ("rb", 128, F32), ("js", 512, BF), ("asl", 128, BF), ("slb", 128, BF), ("dk", 384, BF), ("dkt", 384, BF),
        ("eq", 16, I32), ("ei", 2, I32), ("ef", 4, F32), ("oh", 16, F32), ("hk", 256, BF),
        ("yv0", 128, F32), ("yv1", 128, F32), ("yw0", 256, F32), ("yw1", 256, F32), ("ups", 128, F32),
        ("z", 512, BF), ("dd", 512, BF), ("sx", 128, F32)):
    _buf(_n, _c, _d)
for _n, _c in (("qmb", 160), ("qx", 128), ("qp", 128), ("bb", 128), ("ep", 512), ("en", 512), ("pc", 128), ("qg", 128), ("qk", 128), ("qn", 128), ("qu", 128), ("qw", 256), ("qd", 128),
               ("mw0", 256), ("mw1", 256), ("mw2", 256), ("iw0", 256), ("iw1", 256), ("iw2", 128),
               ("rm0", 32), ("rc0", 64), ("rc1", 64), ("f0", 384), ("f1", 384), ("f2", 384), ("nt", 128)):
    _buf(_n, _c, X4)
    _buf(_n + "_s", _c, U8)
for _t in range(R):
    _buf("ys%d" % _t, 256, F32)
for _t in range(R - 1):
    _buf("lst%d" % _t, 16, U16)
    _buf("rl%d" % _t, 8, U16)
    _buf("rq%d" % _t, 2, U16)

STAGES = ["m0", "m0s", "c0", "c0s", "l0", "c1", "c1s", "l1"]
SEMAPHORES = ["qv", "qs", "qt", "qg", "ls", "lf", "ldr", "ldm", "ldu", "ldw", "hm0", "hc0", "hc1", "hl0", "hl1", "st", "b_l0", "b_l1"]
SEMAPHORES += ["a_" + s for s in STAGES] + ["r_" + s for s in STAGES]
FAR, NEAR = 0, 1


def direct(T, topo, c):
    return [d for d in T.cores if d != c and topo.may_write(c, d)]


def cross(T, topo, c):
    return [d for d in T.cores if d != c and not topo.may_write(c, d)]


def peers(T, topo, c):
    return [x for x in topo.cores_of(c) if T.rank_of(x) is not None]


def relay(T, topo, c, d):
    own = [x for x in topo.cores_of(c) if T.rank_of(x) is None and topo.may_write(x, d)]
    near = [x for x in own if topo.die(x) == topo.die(d)] or own
    same = [x for x in cross(T, topo, c) if topo.die(x) == topo.die(d)]
    return near[same.index(d) % len(near)]


def chips(T, topo, c):
    out = []
    for d in cross(T, topo, c):
        if not out or d not in topo.cores_of(out[-1][0]):
            out.append([])
        out[-1].append(d)
    return out


def runs(T, topo, c):
    out = []
    for r, d in enumerate(T.cores):
        way = NEAR if d == c or topo.may_write(d, c) else FAR
        if out and out[-1][2] == way:
            out[-1][1] += 1
        else:
            out.append([r, 1, way])
    if any(r % 2 for r, _, _ in out):
        out = [[0, N, FAR]]
    return out


def pow2(n):
    k = 1
    while 2 * k <= n:
        k *= 2
    return k


def share(topo, c, dsts):
    off = [d for d in dsts if d not in topo.cores_of(c)]
    on = [d for d in dsts if d in topo.cores_of(c)]
    out = {}
    every = topo.engines(c, on[0]) if on else topo.engines(c, off[0])
    per = pow2(len(every) // len(dsts))
    used = []
    for i, d in enumerate(off):
        out[d] = topo.engines(c, d)[per * i:per * i + per]
        used += out[d]
    left = [e for e in every if e not in used]
    per = pow2(len(left) // len(on)) if on else 0
    for i, d in enumerate(on):
        out[d] = left[per * i:per * i + per]
    return out


def bits(engines):
    return sum(1 << e for e in engines)


def kind(stage):
    return int(stage[1]), "_s" if stage.endswith("s") else "", stage[0] != "l" and not stage.endswith("s"), E if stage[0] == "c" else 0


def roads(T, topo, c, stage, way):
    if way == NEAR:
        out = [(d, [d]) for d in direct(T, topo, c)]
    elif stage[0] == "c":
        out = [(relay(T, topo, c, ds[(j + stage.endswith("s")) % len(ds)]), ds) for j, ds in enumerate(chips(T, topo, c))]
    else:
        out = [(relay(T, topo, c, d), [d]) for d in cross(T, topo, c)]
    e = share(topo, c, [x for x, _ in out])
    return [(x, e[x], ds) for x, ds in out]


def onward(T, topo, x, stage):
    mine = peers(T, topo, x)
    ds = [r[2] for r in roads(T, topo, mine[0], stage, FAR) if r[0] == x] if mine else []
    if not ds:
        return []
    ds = ds[0]
    if len(ds) == 1:
        return [(ds[0], topo.engines(x, ds[0]), 0, len(mine), mine[0])]
    e = topo.engines(x, ds[0])
    per = pow2(len(e) // (len(mine) * len(ds)))
    out = []
    for i, s in enumerate(mine):
        for j, d in enumerate(ds):
            k = len(out)
            out.append((d, e[per * k:per * k + per], i * len(ds) + j, 1, s))
    return out


def arrival(stage, way):
    return ("b_" if stage[0] == "l" and way == FAR else "a_") + stage


def landed(T, topo, c, stage):
    n = {}
    rank = T.rank_of(c) is not None
    for s in T.cores:
        if s != c:
            for way in (FAR, NEAR):
                k = arrival(stage, way) if rank else "r_" + stage
                n[k] = n.get(k, 0) + sum(len(e) for x, e, _ in roads(T, topo, s, stage, way) if x == c)
        if rank and s == peers(T, topo, s)[0] and not topo.may_write(s, c):
            k = arrival(stage, FAR)
            n[k] = n.get(k, 0) + sum(len(o[1]) for x in topo.cores_of(s) if T.rank_of(x) is None for o in onward(T, topo, x, stage) if o[0] == c)
    return n


def view(T, name, a, n, codes):
    x = T[name][:, a:a + n]
    return x.bitcast(dt.uint8) if codes else x


def relay_program(g, core, T, topo):
    total = 0
    for st in STAGES:
        out = onward(T, topo, core, st)
        if not out:
            continue
        t, tail, codes, base = kind(st)
        tr = []
        for d, e, a, n, s in out:
            r = T.rank_of(s)
            if st[0] == "l":
                src, dst = T["rq%d" % t][:, a:a + n], T["rl%d" % t][:, r:r + n]
            else:
                src, dst = view(T, "r" + st[:2] + tail, K * a, K * n, codes), view(T, "iw%d" % t + tail, base + K * r, K * n, codes)
            rid, pid = topo.addr(d, core)
            tr.append(RemoteDMATransfer(dst_ids=[DstId(rid=rid, pnc=pid)], dma_engine_mask=bits(e), remote_sem=T.sem[arrival(st, FAR)], src=src, dst=dst))
            total += len(e)
        g.wait_ge(T.sem["r_" + st], landed(T, topo, core, st)["r_" + st])
        g.remote_dma_fused(tr, local_sem=T.sem["ls"])
    if total:
        g.wait_ge(T.sem["ls"], total)


def rank_program(g, core, T, topo):
    rank = T.rank_of(core)
    if rank is None:
        if peers(T, topo, core):
            relay_program(g, core, T, topo)
        return
    q = {"v": g.vector, "s": g.scalar, "t": g.tensor, "g": g, "y": g.sync}
    count, seen, wrote, read, want = {}, {}, {}, {}, {}

    def need(k, toks):
        for s, n in toks:
            if not (k == "t" and s == "qt") and seen.get((k, s), 0) < n:
                want[s] = max(want.get(s, 0), n)

    def waits(k, rd, wr):
        want.clear()
        for r in rd:
            need(k, wrote.get(r, []))
        for w in wr:
            need(k, wrote.get(w, []))
            need(k, read.get(w, []))
        for s, n in want.items():
            q[k].wait_ge(T.sem[s], n)
            seen[(k, s)] = n

    def note(tok, rd, wr):
        for r in rd:
            read.setdefault(r, []).append(tok)
        for w in wr:
            wrote[w] = [tok]
            read[w] = []

    def op(k, fn, rd=(), wr=()):
        waits(k, rd, wr)
        s = "q" + k
        fn().then_inc(T.sem[s], 1)
        count[s] = count.get(s, 0) + 1
        note((s, count[s]), rd, wr)

    def dmas(parts, s, rd=(), wr=()):
        for k in sorted({p[0] for p in parts}):
            waits(k, rd, wr)
        for k, o, i in parts:
            q[k].dma_start(o, i).then_inc(T.sem[s], 16)
            count[s] = count.get(s, 0) + 16
        note((s, count[s]), rd, wr)

    v, sc, te = g.vector, g.scalar, g.tensor
    u32 = dt.uint32

    def tsc(o, i, s1, s2, o1, o2, rd, wr):
        if o2 is None:
            op("v", lambda: v.tensor_scalar(o, i, s1, None, o1), rd, wr)
        else:
            op("v", lambda: v.tensor_scalar(o, i, s1, s2, o1, o2), rd, wr)

    def cp(o, i, rd, wr):
        op("v", lambda: v.tensor_copy(o, i), rd, wr)

    def ttn(o, a, b, f, rd, wr):
        op("v", lambda: v.tensor_tensor(o, a, b, f), rd, wr)

    def fill(o, x, rd, wr):
        op("v", lambda: v.memset(o, x), rd, wr)

    def turn(o, i, rd, wr):
        op("v", lambda: v.transpose(o, i), rd, wr)

    def act(o, i, fn, rd, wr, **kw):
        op("s", lambda: sc.activation(o, i, fn, **kw), rd, wr)

    def iota(o, pattern, ch, wr, base=0):
        op("g", lambda: g.iota(o, pattern, base, ch, allow_small_or_imprecise_dtypes=True), (), [wr])

    def quant(name, a, b, tile, x, rd, wr):
        op("v", lambda: v.quantize_mx(T[name][:, a:b], T[name + "_s"][:, a:b], T[tile][:, x:x + 4 * (b - a)]), rd, wr)

    def pick(out, a, n, src, c, d, off, e, codes, scales, lists, wc, ws):
        op("v", lambda: v.tensor_copy(T[out][:, a:a + n].bitcast(u32), T[src][:, c:d].bitcast(u32).indirect(T[off][:, e:e + n // K])), codes + lists, [wc])
        op("s", lambda: sc.activation(T[out + "_s"][:, a:a + n], T[src + "_s"][:, c:d].indirect(T[off][:, e:e + n // K]), F.Copy), scales + lists, [ws])

    def mm(bank, ln, la, rn, ra, start, stop, rd):
        op("t", lambda: te.matmul_mx(T[bank][:, 0:128], T[ln][:, la:la + 128], T[ln + "_s"][:, la:la + 128],
                                     T[rn][:, ra:ra + 128], T[rn + "_s"][:, ra:ra + 128], start, stop), rd, [bank])

    parts = []
    for a in range(4):
        for d in range(2):
            parts.append(("ys"[d], T.wr[32 * a + 16 * d:32 * a + 16 * d + 16, 1 - d:9 - d], T.rev[:, :]))
    dmas(parts, "ldr", (), ["wr"])
    dmas([("y", T.mb[:, 0:512], T.m[:, :]), ("s", T.mb[:, 512:640], T.b[:, :])], "ldm", (), ["mb"])
    dmas([("y", T.uc[:, :], T.u[:, 0:4])], "ldu", (), ["uc"])
    dmas([("y", T.wt[:, :], T.w[:, :])], "ldw", (), ["wt"])

    op("g", lambda: g.iota(T.ki[:, 0:2], [[0, 2]], 0, 1), (), ["ip"])
    iota(T.im16[:, :], [[0, 8], [1, 16]], 0, "im16")
    iota(T.t1[:, 32:64], [[128, 2], [0, 16]], 0, "tq")
    iota(T.ij[:, :], [[1, 128]], 0, "ij")
    iota(T.c32[:, :], [[1, 2], [1, 16]], 0, "c32")
    iota(T.mb[:, 640:768], [[0, 128]], 0, "xz")
    iota(T.cf[:, 0:16], [[0, 2], [1, 8]], 0, "c8")
    iota(T.k24[:, :], [[1, 3], [0, 8]], 0, "k24")
    fill(T.eb[:, :], 0.0, (), ["ebz"])
    fill(T.one[:, :], 1.0, (), ["one"])
    tsc(T.ki[:, 2:4], T.ki[:, 0:2], 15, None, A.bitwise_and, None, ["ip"], ["i2"])
    tsc(T.ki[:, 4:6], T.ki[:, 0:2], 4, None, A.logical_shift_right, None, ["ip"], ["i4"])
    tsc(T.ki[:, 6:8], T.ki[:, 0:2], 22, None, A.bitwise_and, None, ["ip"], ["i6"])
    tsc(T.ki[:, 8:10], T.ki[:, 0:2], 5, None, A.logical_shift_right, None, ["ip"], ["i8"])
    cp(T.kf[:, 0:10], T.ki[:, :], ["ip", "i2", "i4", "i6", "i8"], ["kf"])
    tsc(T.kf[:, 11:12], T.ki[:, 8:9], 256.0, BIG, A.mult, A.add, ["i8"], ["kc"])
    tsc(T.t1[:, 0:32], T.t1[:, 32:64], T.kf[:, 11:12], None, A.add, None, ["tq", "kc"], ["t1"])
    tsc(T.kf[:, 10:11], T.ki[:, 2:3], 0.5, None, A.add, None, ["i2"], ["kh"])
    cp(T.ku[:, :], T.ki[:, :], ["ip", "i2", "i4", "i6", "i8"], ["ku"])
    p1, k16, g16, k05 = T.kf[:, 0:1], T.kf[:, 2:3], T.kf[:, 4:5], T.kf[:, 10:11]
    act(T.pa[:, :], T.im16[:, :], F.Abs, ["im16", "kf"], ["pa"], scale=-1.0, bias=k16)
    for i, c in enumerate((0.5, 8.0, 0.5, 0.5)):
        act(T.pw[:, i:512:4], T.pa[:, :], F.Relu, ["pa"], ["pw%d" % i], scale=-c, bias=c)

    def spread(dst, col, rd, both):
        for b in range(4):
            o, x = T[dst][:, 32 * b:32 * b + 32], T.lff[:, col + b:col + b + 1]
            if both and b % 2:
                tsc(o, T.one[:, 0:32], x, None, A.mult, None, ["one", rd], [dst + ".%d" % b])
            else:
                act(o, T.one[:, 0:32], F.Copy, ["one", rd], [dst + ".%d" % b], scale=x)

    tsc(T.lff[:, 0:4], T.wr[:, 1:9:2], 63.75, BIG, A.subtract, A.add, ["wr"], ["h4"])
    for b in range(4):
        tsc(T.ah[:, 32 * b:32 * b + 32], T.t1[:, 0:32], T.lff[:, b:b + 1], None, A.is_equal, None, ["t1", "h4"], ["ah%d" % b])
    turn(T.mk[:, :], T.ah[:, :], ["ah%d" % b for b in range(4)], ["mk"])
    op("v", lambda: v.tensor_tensor_scan(T.cu[:, :], T.mk[:, :], T.mk[:, :], 0.0, A.add, A.max), ["mk"], ["cu"])
    act(T.jk[:, 128:136], T.cu[:, 15:128:16], F.Sign, ["cu", "kh"], ["jb", "acc1"], scale=-1.0, bias=k05, accum_out=T.lff[:, 17:18])
    act(T.jk[:, 0:128], T.cu[:, :], F.Sign, ["cu", "kh"], ["jk", "acc0"], scale=-1.0, bias=k05, accum_out=T.lff[:, 16:17])
    cp(T.lff[:, 4:8], T.wr[:, 1:9:2], ["wr"], ["r4f"])
    quant("qp", 0, 128, "pw", 0, ["pw%d" % i for i in range(4)], ["qp"])
    tsc(T.mb[:, 641:768:4], T.c32[:, :], g16, T.lff[:, 17:18], A.is_equal, A.mult, ["c32", "kf", "acc1", "xz"], ["x1"])
    tsc(T.lff[:, 18:19], T.lff[:, 17:18], -16.0, T.lff[:, 16:17], A.mult, A.add, ["acc0", "acc1"], ["low"])
    tsc(T.mb[:, 640:768:4], T.c32[:, :], g16, T.lff[:, 18:19], A.is_equal, A.mult, ["c32", "kf", "low", "xz"], ["x0"])
    quant("qx", 0, 128, "mb", 256, ["mb", "xz", "x0", "x1"], ["qx"])
    mm("db0", "qp", 0, "qx", 0, True, True, ["qp", "qx"])
    quant("qmb", 0, 160, "mb", 0, ["mb"], ["qmb"])
    spread("ar", 4, "r4f", False)
    act(T.cf[:, 48:64], T.im16[:, 0:16], F.Relu, ["im16", "kf"], ["below"], scale=-1.0, bias=k16)
    act(T.cf[:, 96:112], T.cf[:, 0:16], F.Abs, ["c8", "kf"], ["away"], scale=-1.0, bias=g16)
    act(T.cf[:, 80:96], T.cf[:, 48:64], F.Sign, ["below"], ["lt"])
    act(T.hx[:, 0:16], T.cf[:, 96:112], F.Relu, ["away"], ["hm"], scale=-8.0, bias=8.0)
    act(T.cf[:, 64:80], T.cf[:, 80:96], F.Copy, ["lt"], ["mth"], scale=-2.0 ** -24, bias=1.0)
    act(T.lff[:, 20:24], T.uc[:, :], F.Copy, ["uc"], ["ucf"])
    tsc(T.ls[:, 0:8], T.db0[:, 96:104], 64.0, None, A.add, None, ["db0"], ["ls"])
    pick("mw0", 0, 128, "qmb", 0, 128, "ls", 0, ["qmb"], ["qmb"], ["ls"], "mw0.m", "mw0.m_s")

    def send(stage, way, src, rd, local="ls"):
        t, tail, codes, base = kind(stage)
        i = peers(T, topo, core).index(core)
        waits("g", rd, ())
        tr = []
        for x, e, ds in roads(T, topo, core, stage, way):
            n = len(ds)
            if stage[0] == "l":
                dst = T["rl%d" % t][:, rank:rank + 1] if way == NEAR else T["rq%d" % t][:, i:i + 1]
            elif way == NEAR:
                dst = view(T, "iw%d" % t + tail, base + K * rank, K, codes)
            else:
                dst = view(T, "r" + stage[:2] + tail, K * n * i, K * n, codes)
            rid, pid = topo.addr(x, core)
            tr.append(RemoteDMATransfer(dst_ids=[DstId(rid=rid, pnc=pid)], dma_engine_mask=bits(e),
                                        remote_sem=T.sem[arrival(stage, NEAR) if way == NEAR else "r_" + stage], src=src(T.rank_of(ds[0]), n), dst=dst))
            count[local] = count.get(local, 0) + len(e)
        g.remote_dma_fused(tr, local_sem=T.sem[local])
        count.update(landed(T, topo, core, stage))

    def columns(stage, way, local="ls"):
        t, tail, codes, base = kind(stage)
        m = "mw%d" % t
        send(stage, way, lambda h, n: view(T, m + tail, base + K * h, K * n, codes), [m + (".c" if base else ".m") + tail], local)

    def home(stage, after):
        t, _, _, base = kind(stage)
        m, iw, part, at = "mw%d" % t, "iw%d" % t, ".c" if base else ".m", base + K * rank
        dmas([("y", view(T, iw, at, K, True), view(T, m, at, K, True)),
              ("y", view(T, iw + "_s", at, K, False), view(T, m + "_s", at, K, False))], "h" + stage, [m + part, m + part + "_s"] + after, ["home"])
        h = wrote.pop("home")
        for x, y in (("", ""), ("s", "_s")):
            wrote[iw + part + y] = [("a_" + stage + x, count["a_" + stage + x])] + h

    for way, local in ((FAR, "lf"), (NEAR, "ls")):
        for st in ("m0", "m0s"):
            columns(st, way, local)
    wrote["left"] = [("lf", count["lf"])]
    home("m0", ["left"])
    iota(T.pb[:, :], [[0, 512]], 0, "pb", 1)
    iota(T.nb[:, :], [[0, 516]], 0, "nbz")
    iota(T.gb[:, :], [[0, 512]], 0, "gb")
    iota(T.cf[:, 16:32], [[16, 8], [0, 2]], 0, "h16")

    turn(T.rb[:, :], T.ar[:, :], ["ar.%d" % b for b in range(4)], ["rb"])
    for b in range(4):
        act(T.js[:, 128 * b:128 * b + 128], T.rb[:, :], F.Sign, ["rb", "r4f"], ["js%d" % b, "sa%d" % b], scale=-1.0, bias=T.lff[:, 4 + b:5 + b], accum_out=T.lff[:, 8 + b:9 + b])
    tsc(T.li[:, :], T.db0[:, 96:128], 64.0, None, A.add, None, ["db0"], ["li"])
    cp(T.ld[:, :], T.li[:, :].indirect(T.ku[:, 6:8]), ["li", "ku"], ["ld"])
    tsc(T.l4[:, 24:32], T.li[:, 0:8], 2, None, A.logical_shift_right, None, ["li"], ["l2"])
    tsc(T.l4[:, 0:24], T.ld[:, 0:24], 124, None, A.bitwise_and, None, ["ld"], ["l4"])
    cp(T.ls[:, 8:16], T.l4[:, 24:32], ["l2"], ["lb"])
    ttn(T.fw[:, 0:24], T.l4[:, 0:24], T.k24[:, :], A.add, ["l4", "k24"], ["fw"])
    ttn(T.fw[:, 24:48], T.fw[:, 0:24], T.ld[:, 0:24], A.is_ge, ["fw", "ld"], ["fc"])
    ttn(T.fw[:, 48:72], T.fw[:, 0:24], T.fw[:, 24:48], A.add, ["fw", "fc"], ["fk"])
    cp(T.fd[:, :], T.fw[:, 48:72], ["fk"], ["fd"])
    pick("bb", 0, 128, "qmb", 128, 160, "ls", 8, ["qmb"], ["qmb"], ["lb"], "bb", "bb_s")
    tsc(T.lff[:, 12:16], T.lff[:, 8:12], 0.5, 63.5, A.mult, A.add, ["sa%d" % b for b in range(4)], ["s4"])
    spread("asl", 12, "s4", True)
    tsc(T.eb[:, 3:512:4], T.ij[:, :], p1, None, A.is_equal, None, ["ij", "kf", "ebz"], ["ebh"])
    turn(T.slb[:, :], T.asl[:, :], ["asl.%d" % b for b in range(4)], ["slb"])
    cp(T.dk[:, 0:192], T.slb[:, :].indirect(T.fd[:, 0:12]), ["slb", "fd"], ["dk0"])
    act(T.dk[:, 192:384], T.slb[:, :].indirect(T.fd[:, 12:24]), F.Copy, ["slb", "fd"], ["dk1"])

    def unpacking(b):
        quant("ep", 128 * b, 128 * b + 128, "eb", 3 - b, ["ebz", "ebh"], ["ep%d" % b])

    for b in (0, 1):
        unpacking(b)
    turn(T.dkt[:, :], T.dk[:, :], ["dk0", "dk1"], ["dkt"])
    cp(T.lf[:, :], T.dkt[:, 0:384:16], ["dkt"], ["lf"])
    for b in (2, 3):
        unpacking(b)
    act(T.pb[:, 0:512:4], T.pa[:, :], F.Relu, ["pa", "pb"], ["pb0"], scale=-128.0, bias=128.0)
    act(T.pb[:, 2:512:4], T.im16[:, :], F.Copy, ["im16", "pb"], ["pb2"])

    def tile_u(t):
        act(T.ub[:, t:512:4], T.one[:, :], F.Copy, ["one", "ucf"], ["ub%d" % t], scale=T.lff[:, 20 + t:21 + t])

    for b in (0, 1):
        tile_u(b)

    def prefill_m(t):
        for b in range(4):
            mm("db%d" % b, "en", 128 * b, "mw%d" % t, 0, True, False, ["en%d" % b, "mw%d.m" % t, "mw%d.m_s" % t])

    def prefill_b():
        for b in range(4):
            mm("zb%d" % b, "ep", 128 * b, "bb", 0, True, False, ["ep%d" % b, "bb", "bb_s"])

    prefill_b()
    seg = runs(T, topo, core)
    flags = ["gb", "gb0", "gb1", "gb3", "gb4", "gb5", "gb6", "gb7"]

    def inw(t, tail):
        return ["iw%d.m%s" % (t, tail)] if t == 0 else ["iw%d.m%s.%d" % (t, tail, r) for r, _, _ in seg]

    def results(i, src, m):
        act(T["ys%d" % i][:, 0:128], T[src + "0"][:, 0:128].indirect(T.ln[:, 0:8]), F.Copy, [src + "0" + m, "ln"], ["ys%d.0" % i])
        cp(T["ys%d" % i][:, 128:256], T[src + "1"][:, 0:128].indirect(T.ln[:, 0:8]), [src + "1" + m, "ln"], ["ys%d.1" % i])
        dmas([("y", T.y[:, 256 * i:256 * i + 256], T["ys%d" % i][:, :])], "st", ["ys%d.0" % i, "ys%d.1" % i], ())

    for t in range(R):
        iw, mw, f = "iw%d" % t, "mw%d" % t, "f%d" % t
        nw, last = "mw%d" % (t + 1), t == R - 1
        for k in range(3):
            pick(f, 128 * k, 128, iw, 0, 128, "lf", 8 * k, inw(t, ""), inw(t, "_s"), ["lf"], f + ".%d" % k, f + "s.%d" % k)
        for k in range(3):
            for b in range(4):
                mm("zb%d" % b, "ep", 128 * b, f, 128 * k, False, k == 2, ["ep%d" % b, f + ".%d" % k, f + "s.%d" % k])
        if t == 0:
            tsc(T.nb[:, 3:512:4], T.ij[:, :], p1, -1.0, A.is_equal, A.mult, ["ij", "kf", "nbz"], ["nbh"])
            for b in range(4):
                quant("en", 128 * b, 128 * b + 128, "nb", 3 - b, ["nbz", "nbh"], ["en%d" % b])
            prefill_m(0)
            for b in (2, 3):
                tile_u(b)
            act(T.ub[:, 4:8], T.uc[:, :], F.Copy, ["uc"] + ["ub%d" % b for b in range(4)], ["ubn"], scale=-1.0)
        if t == 1:
            quant("qk", 0, 128, "pk", 0, ["pk%d" % i for i in range(4)], ["qk"])
            quant("qw", 0, 256, "wt", 0, ["wt"], ["qw"])
        if last:
            quant("qn", 0, 128, "pn", 0, ["pnz", "pn0", "pn3"], ["qn"])
            results(1, "yw", ".m")
        for b in range(4):
            if b % 2:
                tsc(T.z[:, b:512:4], T["zb%d" % b][:, 0:128], 0.25, None, A.mult, None, ["zb%d" % b], ["z%d" % b])
            else:
                act(T.z[:, b:512:4], T["zb%d" % b][:, 0:128], F.Copy, ["zb%d" % b], ["z%d" % b], scale=0.25)
        quant(mw, 128, 256, "z", 0, ["z%d" % b for b in range(4)], [mw + ".c", mw + ".c_s"])
        for b in range(4):
            mm("db%d" % b, "ep", 128 * b, mw, 128, False, True, ["ep%d" % b, mw + ".c"])
        if t == 0:
            quant("qu", 0, 128, "ub", 0, ["ubn"] + ["ub%d" % b for b in range(4)], ["qu"])
            quant("pc", 0, 128, "pb", 0, ["pb", "pb0", "pb2"], ["pc"])
            act(T.gb[0:1, 1:32:4], T.one[0:1, 0:8], F.Copy, ["one", "gb"], ["gb1"], scale=float(K * rank))
            act(T.gb[0:1, 33:64:4], T.cf[0:1, 16:32:2], F.Copy, ["h16", "gb"], ["gb3"])
            act(T.gb[0:1, 2:64:4], T.one[0:1, 0:16], F.Copy, ["one", "gb"], ["gb4"])
        if not last:
            for way in (FAR, NEAR):
                for x in ("c%d", "c%ds"):
                    columns(x % t, way)
        for b in range(4):
            if b % 2:
                cp(T.dd[:, b:512:4], T["db%d" % b][:, 0:128], ["db%d" % b], ["dd%d" % b])
            else:
                act(T.dd[:, b:512:4], T["db%d" % b][:, 0:128], F.Copy, ["db%d" % b], ["dd%d" % b])
        quant("qd", 0, 128, "dd", 0, ["dd%d" % b for b in range(4)], ["qd"])
        if last:
            for o in range(O):
                mm("zb%d" % (2 + o), "qw", 128 * o, mw, 128, True, True, ["qw", mw + ".c"])
            cp(T.yw0[:, 128:256], T.zb2[:, 0:128], ["zb2"], ["yw0.c"])
        mm("zb1", "qu", 0, "qd", 0, True, True, ["qu", "qd"])
        mm("zb0", "qd", 0, "qu", 0, True, True, ["qu", "qd"])
        act(T.sx[:, :], T.zb1[:, 0:128], F.Abs, ["zb1"], ["sx"], bias=EPS)
        tsc(T.sm[:, 0:1], T.zb0[:, 0:1], T.zb0[:, 1:2], EPS, A.max, A.add, ["zb0"], ["sc"])
        tsc(T.tt[:, 16:32], T.cf[:, 64:80], T.sm[:, 0:1], None, A.mult, None, ["mth", "sc"], ["th"])
        ttn(T.tt[:, 32:48], T.sx[:, :].indirect(T.ku[:, 0:1]), T.tt[:, 16:32], A.is_gt, ["sx", "ku", "th"], ["kk"])
        op("v", lambda: v.tensor_reduce(T.sm[:, 2:3], T.tt[:, 32:48], AxisListType.X, A.add), ["kk"], ["rk"])
        if t == 0:
            tsc(T.gb[:, 0:64:4], T.hx[:, 0:16], T.sm[:, 2:3], None, A.is_gt, None, ["hm", "rk", "gb"], ["gb0"])
        else:
            tsc(T.gb[:, 0:132:4], T.hx[:, 0:33], T.sm[:, 2:3], None, A.is_gt, None, ["hm", "hn", "h0", "h8", "rk", "gb"], ["gb0"])
        quant("qg", 0, 128, "gb", 0, flags, ["qg"])
        if last:
            act(T.yw1[:, 128:256], T.zb3[:, 0:128], F.Copy, ["zb3"], ["yw1.c"])
            mm("db0", "qk", 0, "qg", 0, True, True, ["qk", "qg"])
            mm("db1", "qg", 0, "qn", 0, True, True, ["qg", "qn"])
            cp(T.ln[:, 8:16], T.db0[:, 16:24], ["db0"], ["nl"])
            pick("nt", 0, 128, mw, 0, 256, "ln", 8, [mw + ".m", mw + ".c"], [mw + ".m_s", mw + ".c_s"], ["nl"], "nt", "nt_s")
            act(T.ys2[:, 0:128], T.yw0[:, :].indirect(T.ln[:, 8:16]), F.Copy, ["yw0.m", "yw0.c", "nl"], ["ys2.0"])
            cp(T.ys2[:, 128:256], T.yw1[:, :].indirect(T.ln[:, 8:16]), ["yw1.m", "yw1.c", "nl"], ["ys2.1"])
            cp(T.ups[:, :], T.db1[:, 0:128], ["db1"], ["ups"])
            dmas([("y", T.oc[:, :], view(T, "nt", 0, 128, True))], "st", ["nt"], ())
            dmas([("y", T.osc[4 * k:4 * k + 4, :], T["nt_s"][32 * k:32 * k + 4, :]) for k in range(4)], "st", ["nt_s"], ())
            dmas([("s", T.y[:, 512:640], T.ys2[:, 0:128])], "st", ["ys2.0"], ())
            dmas([("y", T.y[:, 640:768], T.ys2[:, 128:256])], "st", ["ys2.1"], ())
            dmas([("s", T.up[:, :], T.ups[32:33, :])], "st", ["ups"], ())
            break
        lst = "lst%d" % t
        mm("zb2", "pc", 0, "qg", 0, True, True, ["pc", "qg"])
        if t == 0:
            tsc(T.sm[:, 6:7], T.sm[:, 2:3], 8.0, None, A.is_lt, None, ["rk"], ["cnt"])
        cp(T[lst][:, :], T.zb2[:, 0:16], ["zb2"], [lst])
        for way in (FAR, NEAR):
            send("l%d" % t, way, lambda h, n: T[lst][:, h:h + n], [lst])
        dmas([("y", T["rl%d" % t][:, rank:rank + 1], T[lst][:, rank:rank + 1])], "hl%d" % t, [lst], ["home"])
        h = wrote.pop("home")
        for way in (FAR, NEAR):
            s = arrival("l%d" % t, way)
            wrote["rl%d.%d" % (t, way)] = [(s, count[s])] + (h if way == NEAR else [])
        if len(seg) == 1:
            wrote["rl%d.%d" % (t, FAR)] += wrote["rl%d.%d" % (t, NEAR)]
        home("c%d" % t, [lst])
        pick(nw, 0, 128, mw, 0, 256, lst, 8, [mw + ".m", mw + ".c"], [mw + ".m_s", mw + ".c_s"], [lst], nw + ".m", nw + ".m_s")
        prefill_m(t + 1)
        if t == 0:
            iota(T.pn[:, :], [[0, 512]], 0, "pnz")
            iota(T.hx[:, 24:32], [[0, 8]], 0, "h0")
            iota(T.hx[:, 32:34], [[0, 2]], 0, "h8", 8)
            cp(T.eq[:, :], T.li[:, :].indirect(T.ku[:, 4:5]), ["li", "ku"], ["eq"])
            tsc(T.ei[:, 0:1], T.eq[:, 0:1], 15, None, A.bitwise_and, None, ["eq"], ["e0"])
            tsc(T.ei[:, 1:2], T.eq[:, 0:1], 4, None, A.logical_shift_right, None, ["eq"], ["e1"])
            cp(T.ef[:, 0:2], T.ei[:, :], ["e0", "e1"], ["ef"])
            tsc(T.hk[:, 0:128], T.im16[:, :], T.ef[:, 0:1], None, A.is_equal, None, ["im16", "ef"], ["hk"])
            for i, c in enumerate((128.0, 16.0, 1.0, 1.0)):
                act(T.pk[:, i:512:4], T.hk[:, 0:128], F.Copy, ["hk"], ["pk%d" % i], scale=c)
            cp(T.ef[:, 2:3], T.eq[:, 0:1], ["eq"], ["ee"])
            tsc(T.hk[:, 128:256], T.ij[:, :], T.ef[:, 2:3], None, A.is_equal, None, ["ij", "ee"], ["hnn"])
            for i in (0, 3):
                act(T.pn[:, i:512:4], T.hk[:, 128:256], F.Copy, ["hnn", "pnz"], ["pn%d" % i])
            tsc(T.oh[:, :], T.cf[:, 0:16], T.ef[:, 1:2], None, A.is_equal, None, ["c8", "ef"], ["oh"])
            tsc(T.hx[:, 16:24], T.oh[:, 0:8], 8.0, None, A.mult, None, ["oh"], ["hn"])
            tsc(T.gb[:, 65:128:4], T.oh[:, :], g16, None, A.mult, None, ["oh", "kf", "gb", "qg"], ["gb6"])
            tsc(T.gb[:, 66:128:4], T.oh[:, :], k16, None, A.mult, None, ["oh", "kf", "gb", "qg"], ["gb7"])
        else:
            mm("zb3", "qk", 0, "qg", 0, True, True, ["qk", "qg"])
            for o in range(O):
                mm("zb%d" % o, "qw", 128 * o, mw, 0, True, True, ["qw", mw + ".m", mw + ".m_s"])
            cp(T.ln[:, 0:8], T.zb3[:, 24:32], ["zb3"], ["ln"])
            for o in range(O):
                mm("zb%d" % (2 + o), "qw", 128 * o, nw, 0, True, True, ["qw", nw + ".m", nw + ".m_s"])
            act(T.yv0[:, :], T.zb0[:, 0:128], F.Copy, ["zb0"], ["yv0"])
            cp(T.yv1[:, :], T.zb1[:, 0:128], ["zb1"], ["yv1"])
            act(T.yw0[:, 0:128], T.zb2[:, 0:128], F.Copy, ["zb2"], ["yw0.m"])
            cp(T.yw1[:, 0:128], T.zb3[:, 0:128], ["zb3"], ["yw1.m"])
            results(0, "yv", "")
            tsc(T.gb[:, 131:132], T.sm[:, 2:3], 8.0, T.sm[:, 6:7], A.is_lt, A.add, ["rk", "cnt", "gb"], ["gb5"])
        prefill_b()
        ni = "iw%d" % (t + 1)
        for way in (NEAR, FAR):
            for r, n, w in seg:
                if w == way:
                    pick(ni, K * r, K * n, iw, 0, 256, "rl%d" % t, r, inw(t, "") + [iw + ".c"], inw(t, "_s") + [iw + ".c_s"],
                         ["rl%d.%d" % (t, way)], ni + ".m.%d" % r, ni + ".m_s.%d" % r)
    for s, n in sorted(count.items()):
        g.wait_ge(T.sem[s], n)
